import numpy as np, ml_dtypes
CORES = [35,38,43,46]
N = 4
import mx_ref
BF = ml_dtypes.bfloat16
def gentries(a):
    return np.ascontiguousarray(a.reshape(8, 16, -1).transpose(0, 2, 1)).reshape(8, -1)
def gtable(e):
    e = np.asarray(e); return np.ascontiguousarray(e.reshape(8, -1, 16).transpose(0, 2, 1)).reshape(128, -1).astype(np.int32)
def gcols(t, e):
    v = np.concatenate([t.reshape(8, 16, -1, 4), np.zeros((8, 16, 1, 4), BF)], axis=2)
    return np.ascontiguousarray(np.stack([v[g][:, e[g]] for g in range(8)])).reshape(128, -1)
def tile(rs):
    return np.stack(rs, axis=2).reshape(128, -1).astype(BF)
def pick(q, e):
    c = np.concatenate([q[0].reshape(128, -1, 4), np.zeros((128, 1, 4), np.uint8)], axis=1); s = np.concatenate([q[1], np.ones((16, 1), np.uint8)], axis=1)
    return (np.ascontiguousarray(c[:, e].reshape(128, -1)), np.ascontiguousarray(s[:, e]))
def join(*qs):
    return (np.concatenate([q[0] for q in qs], axis=1), np.concatenate([q[1] for q in qs], axis=1))
def put(q, e, v):
    c, s = q[0].reshape(128, -1, 4).copy(), q[1].copy(); c[:, e] = v[0].reshape(128, -1, 4); s[:, e] = v[1]
    return (c.reshape(128, -1), s)
def pk(c, s):
    return (np.ascontiguousarray(c), mx_ref.live(s))
def emit(q):
    return q[0], q[1]
def packed(v, rng):
    q = [mx_ref.quantize(np.ascontiguousarray(v[r])) for r in range(N)]
    return np.stack([a for a, b in q]), np.stack([mx_ref.plane(b, rng) for a, b in q])
def values_of_codes():
    e, c = np.zeros((128, 128, 4), np.float32), np.zeros((128, 2, 4), np.uint8)
    e[np.arange(128), np.arange(128), 0] = 1
    c[:127, :, 0] = np.arange(256).reshape(2, 128).T[:127]
    return mx_ref.matmul(mx_ref.quantize(e.reshape(128, 512).astype(BF)), (c.reshape(128, 8), np.full((16, 2), 127, np.uint8))).T.reshape(-1).astype(np.float64)
CODE_VALUE, SCALE_VALUE = values_of_codes(), 2.0 ** (np.arange(256) - 127.0)
def decode(q):
    return (CODE_VALUE[q[0]].reshape(16, 8, -1, 4) * SCALE_VALUE[q[1]][:, None, :, None] + 0.0).reshape(128, -1).astype(np.float32)
def f(rng, *shape):
    return mx_ref.flush((rng.standard_normal(shape, dtype=np.float32) * np.exp2(rng.integers(-2, 3, shape[:-1] + (1,)))).astype(BF))
def wide(rng, *shape, cols=0):
    v = rng.standard_normal(shape, dtype=np.float32) * np.exp2(rng.integers(-12, 13, shape)).astype(np.float32)
    if cols: v *= np.repeat(np.exp2(rng.integers(-cols, cols + 1, shape[:-2] + (1, shape[-1] // 4))) * (rng.random(shape[:-2] + (1, shape[-1] // 4)) > 0.0625), 4, axis=-1).astype(np.float32)
    return mx_ref.flush(v.astype(BF))
C, I = 384, 20
DIST = [1, 2]
def big(v):
    v = v.astype(np.float32)
    v[np.abs(v) < np.float32(2.0 ** -16)] = 0
    return v.astype(BF)
def alike(t):
    return np.stack([t] * N)
def lists(t):
    return {"li": np.stack([gtable(t[0][r]) for r in range(N)]), "ri": np.stack([gtable(t[1][r]) for r in range(N)])}
def drawn(rng):
    return lists(rng.integers(0, I, (2, N, 8, C)))
def layers(rng):
    return big(f(rng, 128, 2048)).reshape(8, 16, 4, 8, 16, 4)
def weights(rng, w):
    c, s = packed(alike(np.ascontiguousarray(w).reshape(128, 2048)), rng)
    return {"wc": c, "ws": alike(s[0])}
def setup_inputs(rng):
    return {"x": big(f(rng, N, 128, 4 * C)), "u": alike(np.array(f(rng, 128, 512))), "mid": alike(big(f(rng, 128, 4 * I * I))), "v": np.array(f(rng, N, 128, 512)), **drawn(rng), **weights(rng, layers(rng))}
def scorer(rng):
    u = np.array(f(rng, 128, 512)).reshape(128, 128, 4)
    u[:, ::16] = 0
    return u
def setup_inputs_few(rng):
    d = setup_inputs(rng)
    x = d["x"].reshape(N, 8, 16, C, 4)
    e = rng.permutation(N)
    for r in range(N):
        k = rng.permutation(np.array([0, 1, 2, 3, C // 2 - 1, C // 2, C - 1, C]))
        if r == e[0]: k[:] = 0
        if r == e[1]: k[:] = C
        for g in range(8):
            c = (-rng.integers(0, 2, C)).astype(np.float32)
            c[rng.permutation(C)[:k[g]]] = 1
            x[r, g, 0, :, 0] = c.astype(BF)
    u = scorer(rng)
    for h in range(0, 128, 16): u[h, h, 0] = 1.0
    t = rng.integers(0, I, (2, N, 8, C))
    t[:, e[0]] = I - 1
    t[:, e[1]] = 0
    t[:, e[2]] = rng.integers(0, I, (2, 8, 1))
    w = layers(rng)
    w[:, :, :, :, 0] = 0
    return {"x": x.reshape(N, 128, 4 * C), "u": alike(u.reshape(128, 512)), "mid": d["mid"], "v": d["v"], **lists(t), **weights(rng, w)}
def setup_inputs_near(rng):
    d = setup_inputs(rng)
    x = d["x"].reshape(N, 8, 16, C, 4)
    x[:, :, :8] = 0
    o = rng.permutation(N) % 4
    for r in range(N):
        s = rng.integers(-1, 2, (8, C)).astype(np.float32)
        if o[r] % 2 == 1: s = s[:, np.arange(C) // 16]
        if o[r] < 2: s = s * np.float32(2.0 ** -30)
        for g in rng.permutation(8)[:4]: s[g, rng.integers(C)] = 2.0 ** 29 * rng.choice([-1.0, 1.0])
        x[r, :, 0, :, 0] = s.astype(BF)
    u = scorer(rng)
    small = rng.permutation(8)[:4]
    for g in range(8): u[16 * g, 16 * g, 0] = 2.0 ** -30 if g in small else 1.0
    m = np.array(d["mid"][0]).reshape(8, 16, I * I, 4)
    m[:, :8] = 0
    m[:, 0, :, 0] = 2.0 ** -28
    w = layers(rng)
    w[:, :8] = 0
    w[:, :, :, :, :8] = 0
    return {"x": x.reshape(N, 128, 4 * C), "u": alike(u.reshape(128, 512)), "mid": alike(m.reshape(128, 4 * I * I)), "v": d["v"], **drawn(rng), **weights(rng, w)}
def setup_inputs_fine(rng):
    d = setup_inputs(rng)
    x = d["x"].reshape(N, 8, 16, C, 4)
    x[:, :, :8] = 0
    n = rng.integers(1, 15, (N, 8, C))
    o = rng.permutation(N) % 3
    a = np.stack([n, n + rng.integers(-1, 2, (N, 8, C))], axis=-1) * np.exp2(o - 17.0)[:, None, None, None]
    x[:, :, 0, :, :2] = a.astype(np.float32).astype(BF)
    x[:, :, 1, :, 0] = 1.96875
    x[:, :, 8, :, 0] = 1.0
    u = scorer(rng)
    for h in range(0, 128, 16):
        u[h, h, 0] = 1.0
        u[h, h, 1] = -1.0
    m = np.array(d["mid"][0]).reshape(8, 16, I * I, 4)
    m[:, :8] = 0
    m[:, 8, :, 0] = 1.0
    w = layers(rng)
    w[:, :, :, :, :9] = 0
    w[np.arange(8), 8, 0, np.arange(8), 1, 0] = -1.0
    return {"x": x.reshape(N, 128, 4 * C), "u": alike(u.reshape(128, 512)), "mid": alike(m.reshape(128, 4 * I * I)), "v": d["v"], **drawn(rng), **weights(rng, w)}
def setup_inputs_huge(rng):
    d = setup_inputs(rng)
    h = rng.permutation(8)
    x = -0.98 - 0.02 * rng.random((N, 8, 16, C, 4))
    x[:, h[4:]] = (0.75 + 0.1 * rng.random((N, 4, 16, C, 4))) * rng.choice([-1.0, 1.0], (N, 4, 1, C, 1))
    m = (0.75 + 0.1 * rng.random((8, 16, I * I, 4))) * rng.choice([-1.0, 1.0], (8, 1, I * I, 1))
    u = scorer(rng)
    for g in range(8):
        a = 16 * int(rng.choice(h[4:]))
        u[a:a + 16, 16 * g] = (2.0 ** 30 * (1 - 0.1 * rng.random((16, 4))) * rng.choice([-1.0, 1.0])).astype(np.float32).astype(BF)
    w = np.zeros((128, 4, 128, 4), np.float32)
    i = np.arange(128)
    for b in range(4): w[i, b, i, b] = -1
    return {"x": (2.0 ** 30 * x).astype(np.float32).astype(BF).reshape(N, 128, 4 * C), "u": alike(u.reshape(128, 512)), "mid": alike((2.0 ** 30 * m).astype(np.float32).astype(BF).reshape(128, 4 * I * I)), "v": d["v"], **drawn(rng), **weights(rng, w.astype(BF))}
def setup_inputs_spread(rng):
    d = setup_inputs(rng)
    d["x"] = big(wide(rng, N, 128, 4 * C, cols=6))
    d["mid"] = alike(big(wide(rng, 128, 4 * I * I)))
    return d
def check_inputs(d):
    b = []
    for k in ("x", "u", "mid", "v"):
        a = np.abs(d[k].astype(np.float32))
        if not (np.isfinite(a).all() and ((a == 0) | (a >= 2.0 ** -30) & (a <= 2.0 ** 30)).all()): b.append("a value of " + k)
    for k in ("li", "ri"):
        if not ((d[k] >= 0) & (d[k] < I)).all(): b.append("an entry of " + k)
    for k in ("u", "mid", "wc", "ws"):
        if (d[k] != d[k][:1]).any(): b.append(k + " isn't the same on all ranks")
    if ((d["wc"] & 0x7F) == 0x7F).any(): b.append("a code of wc that is no number")
    none, least, most = [emit(mx_ref.quantize(np.full((128, 16), k, np.float32).astype(BF)))[1][0, 0] for k in (0.0, 2.0 ** -30, 2.0 ** 30)]
    for r in range(N):
        s = mx_ref.live(d["ws"][r])
        if ((s != none) & ((s < least) | (s > most))).any(): b.append("a scale of ws")
    return b
def reference(x, u, mid, v, li, ri, wc, ws):
    qu = [mx_ref.quantize(u[r]) for r in range(N)]
    lay = [pk(wc[r], ws[r]) for r in range(N)]
    third = [decode(mx_ref.quantize(mid[r])).astype(BF) for r in range(N)]
    state = [mx_ref.quantize(x[r]) for r in range(N)]
    left = [gentries(li[r]) for r in range(N)]
    right = [gentries(ri[r]) for r in range(N)]
    mix = np.arange(C).reshape(2, C // 2).T.reshape(-1)
    for d in DIST:
        made, outl, outr = [], [], []
        for r in range(N):
            s = mx_ref.matmul(qu[r], state[r])[::16]
            o = np.argsort(~(s > 0), axis=1, kind="stable")
            l, h = o[:, ::2], o[:, 1::2]
            full = decode(state[r]).astype(BF)
            most = np.maximum(gcols(full, l).astype(np.float32), gcols(full, h).astype(np.float32))
            n = I * np.take_along_axis(right[r], l, axis=1) + np.take_along_axis(left[r], h, axis=1)
            z = mx_ref.quantize(((most + gcols(third[r], n).astype(np.float32)) * np.float32(0.5)).astype(BF))
            made.append(mx_ref.quantize(tile([mx_ref.matmul(pick(lay[r], np.arange(128 * b, 128 * b + 128)), z) * np.float32(0.03125) + most[:, b::4] for b in range(4)])))
            outl.append(np.take_along_axis(left[r], l, axis=1))
            outr.append(np.take_along_axis(right[r], h, axis=1))
        for r in range(N):
            e = (r - d) % N
            state[r] = pick(join(made[e], made[r]), mix)
            left[r] = np.concatenate([outl[e], outl[r]], axis=1)[:, mix]
            right[r] = np.concatenate([outr[e], outr[r]], axis=1)[:, mix]
    y, lr = np.zeros((N, 128, C), np.float32), np.zeros((N, 8, 2 * C), np.float32)
    oc, osc = np.zeros((N, 128, 4 * C), np.uint8), np.zeros((N, 16, C), np.uint8)
    for r in range(N):
        y[r] = mx_ref.matmul(mx_ref.quantize(v[r]), state[r])
        lr[r] = np.concatenate([left[r], right[r]], axis=1)
        oc[r], osc[r] = emit(state[r])
    return {"y": y, "lr": lr, "oc": oc, "osc": osc}

@@ -1,0 +1,370 @@
+from concourse.bass import DstId, RemoteDMATransfer
+from concourse.mybir import dt, AluOpType, ActivationFunctionType
+
+C = 384
+H = C // 2
+NM = 400
+I = 20
+HALF = "float16"
+X4 = "float8_e4m3fn_x4"
+K = 512.0
+B16 = 1024.0
+B4 = 4194304.0
+AW = 2048.0
+
+
+def _sb(n, d):
+    return ("sbuf", [128, n], d)
+
+
+SCRATCH = {
+    "ps": ("psum", [128, 4096], "float32"),
+    "xs": _sb(4 * C, "bfloat16"), "us": _sb(512, "bfloat16"), "vs": _sb(512, "bfloat16"), "ms": _sb(4 * NM, "bfloat16"),
+    "q1": _sb(C, X4), "s1": _sb(C, "uint8"), "q2": _sb(C, X4), "s2": _sb(C, "uint8"), "q3": _sb(C, X4), "s3": _sb(C, "uint8"),
+    "qo": _sb(C, X4), "so": _sb(C, "uint8"),
+    "qu": _sb(128, X4), "su": _sb(128, "uint8"), "qr": _sb(128, X4), "sr": _sb(128, "uint8"),
+    "qv": _sb(128, X4), "sv": _sb(128, "uint8"), "qm": _sb(NM, X4), "sm": _sb(NM, "uint8"),
+    "qw": _sb(512, X4), "sw": _sb(512, "uint8"), "qe": _sb(512, X4), "se": _sb(512, "uint8"),
+    "eb": _sb(520, "bfloat16"), "idm": _sb(128, "float32"),
+    "pcol": _sb(1, "int32"), "ci": _sb(8, "int32"), "cf": _sb(8, "float32"), "cd": _sb(16, "float32"),
+    "j16": _sb(72, "float32"), "j2": _sb(24, "float32"), "r17": _sb(17, "float32"), "base": _sb(C, "int32"),
+    "dt1": _sb(64, "float32"), "d16s": _sb(16, "bfloat16"), "d4s": _sb(16, "bfloat16"),
+    "d16": _sb(C, "bfloat16"), "d4": _sb(H, "bfloat16"),
+    "offu": _sb(8, "uint16"), "offi": _sb(24, "uint16"), "offt": _sb(12, "uint16"), "offx": _sb(24, "uint16"), "offf": _sb(24, "uint16"),
+    "lab": _sb(144, "int32"), "lt": _sb(216, "float32"), "jc": _sb(72, "float32"), "jb1": _sb(24, "float32"), "jb2": _sb(24, "float32"),
+    "xg": _sb(C, "float32"), "val1": _sb(C, "float32"), "val2": _sb(C, "int32"),
+    "mf": _sb(4 * NM, "bfloat16"),
+    "iw": _sb(C, "int32"), "xa": _sb(H, "int32"), "xb": _sb(H, "int32"), "xc": _sb(H, "int32"),
+    "wd": _sb(C, "float32"), "lw": _sb(24, "float32"), "lwr": _sb(24, "float32"),
+    "lri": _sb(48, "int32"), "lrj": _sb(48, "int32"), "lrf": _sb(48, "float32"),
+    "yb": _sb(C, "float32"),
+}
+for _r in ("1", "2"):
+    SCRATCH.update({
+        "f" + _r: _sb(4 * C, "bfloat16"), "fb" + _r: _sb(2 * C + 2, HALF), "ys" + _r: _sb(C + 2, HALF), "yh" + _r: _sb(C, HALF),
+        "sm" + _r: _sb(80, "float32"), "pos" + _r: _sb(24, "uint16"), "w" + _r: _sb(C, "float32"), "hw" + _r: _sb(C, "float32"),
+        "ol" + _r: _sb(48, "uint16"), "oh" + _r: _sb(48, "uint16"), "om" + _r: _sb(48, "uint16"),
+        "im" + _r: _sb(192, "int32"), "fm" + _r: _sb(96, "float32"),
+        "fh" + _r: _sb(4 * H, "bfloat16"), "p" + _r: _sb(4 * H, "bfloat16"), "pp" + _r: _sb(4 * H, "bfloat16"),
+        "z" + _r: _sb(4 * H, "bfloat16"), "t" + _r: _sb(4 * H, "bfloat16"), "vt" + _r: _sb(4 * H, "bfloat16"),
+        "qz" + _r: _sb(H, X4), "sz" + _r: _sb(H, "uint8"),
+    })
+NSEM = 140
+SEMAPHORES = ["e%d" % k for k in range(NSEM)] + ["rq1", "rq2", "rl1", "rl2", "sent"]
+
+AL = AluOpType
+AF = ActivationFunctionType
+
+
+def rank_program(g, core, T, topo):
+    rank = T.rank_of(core)
+    if rank is None:
+        return
+    n = len(T.cores)
+    queues = {"V": g.vector, "A": g.scalar, "P": g.tensor, "S": g.sync, "G": g}
+    waited = {k: {} for k in queues}
+    pool = {k: [] for k in queues}
+    count = {}
+    order = []
+
+    def wait(e, ev):
+        if waited[e].get(ev[0], 0) < ev[1]:
+            queues[e].wait_ge(T.sem[ev[0]], ev[1])
+            waited[e][ev[0]] = ev[1]
+
+    def fresh():
+        name = "e%d" % len(order)
+        order.append(name)
+        count[name] = 0
+        return name
+
+    def op(e, call, deps=()):
+        for d in deps:
+            wait(e, d)
+        name = None
+        for s in pool[e]:
+            if waited[e].get(s, 0) >= count[s]:
+                name = s
+                break
+        if name is None:
+            name = fresh()
+            pool[e].append(name)
+        call(queues[e]).then_inc(T.sem[name], 1)
+        count[name] += 1
+        return (name, count[name])
+
+    def dma(e, out, in_, deps=()):
+        for d in deps:
+            wait(e, d)
+        name = fresh()
+        queues[e].dma_start(out, in_).then_inc(T.sem[name], 16)
+        count[name] = 16
+        return (name, 16)
+
+    def ts(out, in0, a, b, o0, o1=None, deps=()):
+        if o1 is None:
+            return op("V", lambda q: q.tensor_scalar(out, in0, a, None, o0), deps)
+        return op("V", lambda q: q.tensor_scalar(out, in0, a, b, o0, o1), deps)
+
+    def tt(out, in0, in1, o, deps=()):
+        return op("V", lambda q: q.tensor_tensor(out, in0, in1, o), deps)
+
+    def cp(out, in_, deps=()):
+        return op("V", lambda q: q.tensor_copy(out, in_), deps)
+
+    def scan(out, d0, d1, init, o0, o1, deps=()):
+        return op("V", lambda q: q.tensor_tensor_scan(out, d0, d1, init, o0, o1), deps)
+
+    def quant(out, sc, in_, deps=()):
+        return op("V", lambda q: q.quantize_mx(out, sc, in_), deps)
+
+    def fill(ap, c):
+        return op("V", lambda q: q.memset(ap, c))
+
+    def act(out, in_, scale=1.0, bias=None, deps=()):
+        if bias is None:
+            if isinstance(scale, float) and scale == 1.0:
+                return op("A", lambda q: q.activation(out, in_, AF.Copy), deps)
+            return op("A", lambda q: q.activation(out, in_, AF.Copy, scale=scale), deps)
+        return op("A", lambda q: q.activation(out, in_, AF.Identity, bias=bias, scale=scale), deps)
+
+    def mm(bank, w, sw, x, sx, m, deps=()):
+        return op("P", lambda q: q.matmul_mx(T.ps[:, 512 * bank:512 * bank + m], w, sw, x, sx, True, True), deps)
+
+    def iota(out, pattern, base, cm, flt):
+        if flt:
+            return op("G", lambda q: q.iota(out, pattern, base, cm, allow_small_or_imprecise_dtypes=True))
+        return op("G", lambda q: q.iota(out, pattern, base, cm))
+
+    def bank(b, m):
+        return T.ps[:, 512 * b:512 * b + m]
+
+    dst = [T.cores[(rank + 1) % n], T.cores[(rank + 2) % n]]
+    src = [T.cores[(rank - 1) % n], T.cores[(rank - 2) % n]]
+
+    def lanes(c):
+        r = T.rank_of(c)
+        return topo.mask(c, T.cores[(r + 1) % n]) & topo.mask(c, T.cores[(r + 2) % n])
+
+    def width(c):
+        return bin(lanes(c)).count("1")
+
+    sent = [0]
+
+    def push(k, out, in_, sem, deps):
+        for d in deps:
+            wait("G", d)
+        rid, pid, _e = topo.addr(dst[k])
+        g.remote_dma(out, in_, T.sem[sem], T.sem["sent"], pid, rid, lanes(core))
+        sent[0] += width(core)
+
+    z_lab = fill(T.lab[:], 0)
+    l_x0 = dma("S", T.xs[:, 0:2 * C], T.x[:, 0:2 * C])
+    l_x1 = dma("S", T.xs[:, 2 * C:4 * C], T.x[:, 2 * C:4 * C])
+    l_u = dma("A", T.us[:], T.u[:])
+    l_l = []
+    for e, t, o in (("A", T.li, 0), ("S", T.ri, 72)):
+        l_l.append(dma(e, T.lab[:, o:o + 24], t[:], [z_lab]))
+        l_l.append(dma(e, T.lab[16:128, o + 24:o + 48], t[0:112, :], [z_lab]))
+        l_l.append(dma(e, T.lab[0:112, o + 48:o + 72], t[16:128, :], [z_lab]))
+    l_m = dma("S", T.ms[:], T.mid[:])
+    l_w = dma("S", T.qw[:].bitcast(dt.uint8), T.wc[:], [l_x1])
+    l_ws = dma("S", T.sw[:], T.ws[:])
+    l_v = dma("S", T.vs[:], T.v[:])
+
+    g_p = iota(T.pcol[:], [[0, 1]], 0, 1, False)
+    g_j = iota(T.j16[:], [[0, 3], [16, 24]], 0, 0, True)
+    g_r = iota(T.r17[:], [[1, 17]], -1, 0, True)
+    g_i = iota(T.idm[:], [[1, 128]], 0, -1, True)
+    g_j2 = iota(T.j2[:], [[1, 2], [32, 12]], 0, 0, True)
+    g_b = iota(T.base[:], [[int(4 * AW), C]], 0, 0, False)
+
+    z_e = fill(T.eb[:], 0.0)
+    z_f = [fill(T.fb1[:, C:C + 1], 0.0), None]
+    c0 = ts(T.ci[:, 0:1], T.pcol[:], 15, None, AL.bitwise_and, None, [g_p])
+    c1 = ts(T.ci[:, 1:2], T.pcol[:], 3, None, AL.bitwise_and)
+    c2 = ts(T.ci[:, 2:3], T.pcol[:], 2, 3, AL.logical_shift_right, AL.bitwise_and)
+    c3 = ts(T.ci[:, 3:4], T.pcol[:], 4, 1, AL.logical_shift_right, AL.bitwise_and)
+    k_u = cp(T.offu[:], T.j16[:, 0:8], [g_j])
+    k_c = cp(T.cf[:, 0:4], T.ci[:, 0:4], [c0, c1, c2, c3])
+    ci_, ct_, cs_, ce_ = T.cf[:, 0:1], T.cf[:, 1:2], T.cf[:, 2:3], T.cf[:, 3:4]
+    nb_, t4_, i8_, jb1_, c4_, e25_, e47_, jb2_, fq_, lm_, la_ = [T.cd[:, k:k + 1] for k in range(11)]
+    k_e = ts(T.eb[:, 3:515:4], T.idm[:], 0.0, None, AL.is_equal, None, [g_i, z_e])
+    a_e25 = act(e25_, ce_, 25.0, None, [k_c])
+    a_e47 = act(e47_, ce_, -47.0, 48.0)
+    a_i8 = act(i8_, ci_, 4 * AW)
+    k_nb = ts(nb_, ci_, 15.0, -B16, AL.is_lt, AL.mult, [k_c])
+    k_t4 = ts(t4_, cs_, 3.0, -B4, AL.is_lt, AL.mult)
+    k_a = ts(T.dt1[:, 0:16], T.r17[:, 1:17], ci_, -2 * B16, AL.is_equal, AL.mult, [g_r])
+    k_b = ts(T.dt1[:, 16:32], T.r17[:, 0:16], ci_, B16, AL.is_equal, AL.mult)
+    k_a4 = ts(T.dt1[:, 32:48], T.r17[:, 1:17], cs_, -2 * B4, AL.is_equal, AL.mult)
+    k_b4 = ts(T.dt1[:, 48:64], T.r17[:, 0:16], cs_, B4, AL.is_equal, AL.mult)
+    k_oi = ts(T.offi[:], T.j16[:, 0:24], 0.0, ci_, AL.mult, AL.add)
+    k_ot = ts(T.offt[:], T.j16[:, 0:12], 0.0, ct_, AL.mult, AL.add)
+    k_d16 = tt(T.d16s[:], T.dt1[:, 0:16], T.dt1[:, 16:32], AL.add, [k_a, k_b])
+    k_d4 = tt(T.d4s[:], T.dt1[:, 32:48], T.dt1[:, 48:64], AL.add, [k_a4, k_b4])
+    k_x0 = ts(T.offx[:, 0:24:2], T.j16[:, 0:12], 0.125, e25_, AL.mult, AL.add, [a_e25])
+    k_x1 = ts(T.offx[:, 1:24:2], T.j16[:, 0:12], 0.125, e47_, AL.mult, AL.add, [a_e47])
+    a_jc = act(T.jc[:], T.j16[:], 4 * AW, i8_, [a_i8, g_j])
+    a_jb = act(jb1_, nb_, -2.0, ci_, [k_nb])
+    a_c4 = act(c4_, ct_, AW, t4_, [k_t4])
+    a_jb1 = act(T.jb1[:], T.j16[:, 0:24], 1.0, jb1_, [a_jb])
+    a_d16 = act(T.d16[:], T.d16s[:].indirect(T.offi[:]), 1.0, None, [k_d16, k_oi])
+    a_d4 = act(T.d4[:], T.d4s[:].indirect(T.offt[:]), 1.0, None, [k_d4, k_ot])
+    q_e = [quant(T.qe[:, 128 * b:128 * b + 128], T.se[:, 128 * b:128 * b + 128], T.eb[:, 3 - b:515 - b], [k_e]) for b in range(4)]
+
+    q_u = quant(T.qu[:], T.su[:], T.us[:], [l_u])
+    p_u = cp(T.qr[:].bitcast(dt.uint32), T.qu[:].bitcast(dt.uint32).indirect(T.offu[:]), [q_u, k_u])
+    p_us = act(T.sr[:], T.su[:].indirect(T.offu[:]), 1.0, None, [q_u, k_u])
+    v_1 = ts(T.lt[:, 0:72], T.lab[:, 72:144], 32.0, None, AL.mult, None, l_l[3:])
+    v_2 = tt(T.lt[:, 72:144], T.lab[:, 0:72], T.jc[:], AL.add, l_l[:3] + [a_jc])
+    q_x0 = quant(T.q1[:, 0:H], T.s1[:, 0:H], T.xs[:, 0:2 * C], [l_x0])
+    v_3 = tt(T.lt[:, 144:216], T.lt[:, 0:72], T.lt[:, 72:144], AL.add, [v_1, v_2])
+    q_x1 = quant(T.q1[:, H:C], T.s1[:, H:C], T.xs[:, 2 * C:4 * C], [l_x1])
+    a_x = act(T.xg[:], T.lt[:, 144:216].indirect(T.offx[:]), 1.0, None, [v_3, k_x0, k_x1])
+
+    def unpack(q, s, m, banks, deps):
+        return [mm(banks[b], T.qe[:, 128 * b:128 * b + 128], T.se[:, 128 * b:128 * b + 128], q, s, m, deps[b] + [q_e[b]]) for b in range(4)]
+
+    def evac(f, lo, m, banks, evs):
+        return [act(f[:, lo + b:lo + 4 * m:4], bank(banks[b], m), 0.5, None, [evs[b]]) for b in range(4)]
+
+    def flags(r, b, lo, step, m, deps):
+        fb = T["fb" + r]
+        f1 = ts(fb[:, lo:C:step], bank(b, m), 0.0, K, AL.is_gt, AL.mult, deps)
+        f2 = ts(fb[:, C + 1 + lo:2 * C + 1:step], fb[:, lo:C:step], (K + 1) / K, None, AL.mult, None, [f1])
+        return [f1, f2]
+
+    def places(r, fl, jb, jdeps, val, vdeps):
+        fb, ys, yh, sm = T["fb" + r], T["ys" + r], T["yh" + r], T["sm" + r]
+        s = scan(ys[:, 0:C + 1], fb[:, C:2 * C + 1], fb[:, 0:C + 1], K, AL.add, AL.subtract, fl)
+        tc = cp(sm[:, 72:73], ys[:, C:C + 1], [s])
+        if r == "1":
+            hs = [scan(yh[:], T.d16[:], ys[:, 0:C], 0.0, AL.add, AL.max, [s, a_d16])]
+        else:
+            hs = [scan(yh[:, H * k:H * k + H], T.d16[:, 0:H], ys[:, k:C:2], 0.0, AL.add, AL.max, [s, a_d16]) for k in range(2)]
+        jt = ts(sm[:, 0:24], jb, sm[:, 72:73], None, AL.add, None, [tc] + jdeps)
+        d = tt(sm[:, 24:48], sm[:, 0:24], yh[:, 15:C:16], AL.subtract, [jt] + hs)
+        mn = tt(sm[:, 48:72], sm[:, 24:48], yh[:, 15:C:16], AL.min, [d])
+        po = ts(T["pos" + r][:], sm[:, 48:72], nb_, None, AL.add, None, [mn, k_nb])
+        return cp(T["w" + r][:].indirect(T["pos" + r][:]), val, [po] + vdeps)
+
+    def layer(r, sc, fdeps, mdeps, bdeps, between, gap, q, s):
+        w, hw, im, fm = T["w" + r], T["hw" + r], T["im" + r], T["fm" + r]
+        ol, oh, om = T["ol" + r], T["oh" + r], T["om" + r]
+        f, fh, p, pp, z, t, vt = [T[x + r] for x in ("f", "fh", "p", "pp", "z", "t", "vt")]
+        sh = scan(hw[:, H:C], T.d4[:], w[:, 1:C:2], 0.0, AL.add, AL.max, [sc, a_d4])
+        sl = scan(hw[:, 0:H], T.d4[:], w[:, 0:C:2], 0.0, AL.add, AL.max, [sc])
+        oh_ = ts(oh[:], hw[:, H + 3:C:4], c4_, 1.0 / AW, AL.add, AL.mult, [sh, a_c4])
+        gh = [act(fh[:, C * k:C * k + C], f[:].indirect(oh[:, 24 * k:24 * k + 24]), 1.0, None, [oh_] + fdeps) for k in range(2)]
+        between()
+        i0 = cp(im[:, 0:96], hw[:, 3:C:4], [sh, sl])
+        ol_ = ts(ol[:], hw[:, 3:H:4], c4_, 1.0 / AW, AL.add, AL.mult, [sl])
+        i1 = ts(im[:, 96:144], im[:, 0:48], 31 * 32, None, AL.bitwise_and, None, [i0])
+        i2 = ts(im[:, 144:192], im[:, 48:96], 31, None, AL.bitwise_and, None, [i0])
+        i3 = ts(fm[:, 0:48], im[:, 96:144], I / 32.0, None, AL.mult, None, [i1])
+        i4 = tt(fm[:, 48:96], fm[:, 0:48], im[:, 144:192], AL.add, [i3, i2])
+        om_ = ts(om[:], fm[:, 48:96], 4.0, ct_, AL.mult, AL.add, [i4])
+        mx = [tt(p[:, C * k:C * k + C], f[:].indirect(ol[:, 24 * k:24 * k + 24]), fh[:, C * k:C * k + C], AL.max, [ol_, gh[k]] + fdeps)
+              for k in range(2)]
+        a_p = act(pp[:], p[:], 64.0, None, mx)
+        zz = tt(z[:], T.mf[:].indirect(om[:]), p[:], AL.add, mx + [om_] + mdeps())
+        qz = quant(T["qz" + r][:], T["sz" + r][:], z[:], [zz])
+        rr = [mm(1 + b, T.qw[:, 128 * b:128 * b + 128], T.sw[:, 128 * b:128 * b + 128], T["qz" + r][:], T["sz" + r][:], H,
+                 [qz, l_w, l_ws] + bdeps) for b in range(4)]
+        gap()
+        ad = [tt(t[:, b:4 * H:4], bank(1 + b, H), pp[:, b:4 * H:4], AL.add, [rr[b], a_p]) for b in range(4)]
+        sv = [act(vt[:, b:4 * H:4], t[:, b:4 * H:4], 0.03125, None, [ad[b]]) for b in range(3)]
+        sv.append(ts(vt[:, 3:4 * H:4], t[:, 3:4 * H:4], 0.03125, None, AL.mult, None, [ad[3]]))
+        return quant(q, s, vt[:], sv), ad
+
+    m_s = mm(0, T.qr[:], T.sr[:], T.q1[:], T.s1[:], C, [p_u, p_us, q_x0, q_x1])
+    m_d = unpack(T.q1[:], T.s1[:], C, [1, 2, 3, 4], [[]] * 4)
+    q_m = quant(T.qm[:], T.sm[:], T.ms[:], [l_m])
+    fl = flags("1", 0, 0, 1, C, [m_s])
+    e_f = evac(T.f1, 0, C, [1, 2, 3, 4], m_d)
+    m_m = unpack(T.qm[:], T.sm[:], NM, [5, 6, 7, 0], [[q_m]] * 3 + [[fl[0]]])
+    tr = op("V", lambda q: q.transpose(T.val1[:], T.xg[:]), [a_x])
+    e_m = [act(T.mf[:, b:4 * NM:4], bank([5, 6, 7, 0][b], NM), 0.5, None, [m_m[b]]) for b in range(2)]
+    sc = places("1", fl + [z_f[0]], T.jb1[:], [a_jb1], T.val1[:], [tr])
+
+    def between1():
+        for b in (2, 3):
+            e_m.append(act(T.mf[:, b:4 * NM:4], bank([5, 6, 7, 0][b], NM), 0.5, None, [m_m[b]]))
+
+    keep = {}
+
+    def gap1():
+        i0 = cp(T.iw[:], T.w1[:], [sc])
+        keep["xa"] = ts(T.xa[:], T.iw[:, 0:C:2], 31, None, AL.bitwise_and, None, [i0])
+        keep["xb"] = ts(T.xb[:], T.iw[:, 1:C:2], 31 * 32, None, AL.bitwise_and, None, [i0])
+        for d in (keep["xa"], keep["xb"], g_b):
+            wait("G", d)
+        rid, pid, _e = topo.addr(dst[0])
+        g.remote_dma_fused([RemoteDMATransfer(dst_ids=[DstId(rid=rid, pnc=pid)], dma_engine_mask=lanes(core), remote_sem=T.sem["rl1"],
+                                              srcs=[T.xa[:], T.xb[:], T.base[:, 0:H]], dsts=[T.val2[:, 0:H]], alu_op=1)],
+                           local_sem=T.sem["sent"])
+        sent[0] += width(core)
+
+    q_v1, ad1 = layer("1", sc, e_f, lambda: e_m, e_f, between1, gap1, T.q2[:, H:C], T.s2[:, H:C])
+    push(0, T.q2[:, 0:H].bitcast(dt.uint8), T.q2[:, H:C].bitcast(dt.uint8), "rq1", [q_v1])
+    push(0, T.s2[:, 0:H], T.s2[:, H:C], "rq1", [q_v1])
+
+    m_so = mm(5, T.qr[:], T.sr[:], T.q2[:, H:C], T.s2[:, H:C], H, [q_v1, e_m[0]])
+    m_do = unpack(T.q2[:, H:C], T.s2[:, H:C], H, [1, 2, 3, 4], [[]] * 4)
+    z_f[1] = fill(T.fb2[:, C:C + 1], 0.0)
+    k_jb = ts(jb2_, ci_, nb_, 2.0, AL.subtract, AL.mult, [k_nb])
+    o_1 = tt(T.xc[:], T.xa[:], T.xb[:], AL.add, [keep["xa"], keep["xb"]])
+    flo = flags("2", 5, 1, 2, H, [m_so])
+    k_jb2 = ts(T.jb2[:], T.j2[:], jb2_, None, AL.add, None, [k_jb, g_j2])
+    o_2 = tt(T.val2[:, H:C], T.xc[:], T.base[:, H:C], AL.add, [o_1, g_b])
+    q_v = quant(T.qv[:], T.sv[:], T.vs[:], [l_v])
+    e_o = evac(T.f2, 4 * H, H, [1, 2, 3, 4], m_do)
+
+    r1 = ("rq1", 2 * width(src[0]))
+    m_sa = mm(6, T.qr[:], T.sr[:], T.q2[:, 0:H], T.s2[:, 0:H], H, [r1, e_m[1]])
+    m_da = unpack(T.q2[:, 0:H], T.s2[:, 0:H], H, [1, 2, 3, 4], [[e] for e in e_o])
+    fla = flags("2", 6, 0, 2, H, [m_sa])
+    e_a = evac(T.f2, 0, H, [1, 2, 3, 4], m_da)
+    sc2 = places("2", fla + flo + [z_f[1]], T.jb2[:], [k_jb2], T.val2[:], [o_2, ("rl1", width(src[0]))])
+
+    def between2():
+        a0 = act(T.wd[:, 0:H], T.w2[:, 0:C:2], 1.0, None, [sc2])
+        a1 = act(T.wd[:, H:C], T.w2[:, 1:C:2], 1.0, None, [sc2])
+        keep["lw"] = dma("S", T.lw[:], T.wd[0:128:16, :], [a0, a1])
+        push(1, T.lwr[:], T.lw[:], "rl2", [keep["lw"]])
+
+    q_v2, ad2 = layer("2", sc2, e_o + e_a, lambda: [], e_a, between2, lambda: None, T.q3[:, H:C], T.s3[:, H:C])
+    push(1, T.q3[:, 0:H].bitcast(dt.uint8), T.q3[:, H:C].bitcast(dt.uint8), "rq2", [q_v2])
+    push(1, T.s3[:, 0:H], T.s3[:, H:C], "rq2", [q_v2])
+
+    m_yo = mm(5, T.qv[:], T.sv[:], T.q3[:, H:C], T.s3[:, H:C], H, [q_v2, q_v, flo[0]])
+    c4 = ts(T.ci[:, 4:5], T.pcol[:], 3, 1, AL.logical_shift_right, AL.bitwise_and)
+    c5 = ts(T.ci[:, 5:6], T.pcol[:], 1, None, AL.bitwise_and)
+    c6 = ts(T.ci[:, 6:7], T.pcol[:], 1, 7, AL.logical_shift_right, AL.bitwise_and)
+    k_c2 = cp(T.cf[:, 4:7], T.ci[:, 4:7], [c4, c5, c6])
+    k_lm = ts(lm_, T.cf[:, 4:5], -31.0 / 32.0, 1.0, AL.mult, AL.add, [k_c2])
+    k_la = ts(la_, T.cf[:, 4:5], -0.3, None, AL.mult)
+    k_fq = ts(fq_, T.cf[:, 5:6], float(H), T.cf[:, 6:7], AL.mult, AL.add)
+    k_of = ts(T.offf[:], T.j16[:, 0:24], 0.5, fq_, AL.mult, AL.add, [k_fq])
+    u_0 = ts(T.lri[:, 1:48:2], T.lw[:], lm_, la_, AL.mult, AL.add, [k_lm, k_la, keep["lw"]])
+    u_1 = ts(T.lri[:, 0:48:2], T.lwr[:], lm_, la_, AL.mult, AL.add, [("rl2", width(src[1]))])
+    u_2 = ts(T.lrj[:], T.lri[:], 31, None, AL.bitwise_and, None, [u_0, u_1])
+    u_3 = cp(T.lrf[:], T.lrj[:], [u_2])
+    dma("S", T.lr[:], T.lrf[:], [u_3])
+    y_o = act(T.yb[:, 1:C:2], bank(5, H), 1.0, None, [m_yo])
+
+    r2 = ("rq2", 2 * width(src[1]))
+    m_ya = mm(6, T.qv[:], T.sv[:], T.q3[:, 0:H], T.s3[:, 0:H], H, [r2, fla[0]])
+    p_c = cp(T.qo[:].bitcast(dt.uint32), T.q3[:].bitcast(dt.uint32).indirect(T.offf[:]), [r2, q_v2, k_of])
+    y_a = act(T.yb[:, 0:C:2], bank(6, H), 1.0, None, [m_ya])
+    dma("S", T.y[:], T.yb[:], [y_a, y_o])
+    p_s = act(T.so[:], T.s3[:].indirect(T.offf[:]), 1.0, None, [r2, q_v2, k_of])
+    dma("S", T.oc[:], T.qo[:].bitcast(dt.uint8), [p_c])
+    for k in range(4):
+        dma("A" if k % 2 == 0 else "S", T.osc[4 * k:4 * k + 4, :], T.so[32 * k:32 * k + 4, :], [p_s])
+
+    wait("G", ("sent", sent[0]))
+    for name in order:
+        if max(waited[e].get(name, 0) for e in queues) < count[name]:
+            wait("G", (name, count[name]))

@@ -27,8 +27,8 @@ SCRATCH = {
     "qw": _sb(512, X4), "sw": _sb(512, "uint8"), "qe": _sb(512, X4), "se": _sb(512, "uint8"),
     "eb": _sb(520, "bfloat16"), "idm": _sb(128, "float32"),
     "pcol": _sb(1, "int32"), "ci": _sb(8, "int32"), "cf": _sb(8, "float32"), "cd": _sb(16, "float32"),
-    "j16": _sb(72, "float32"), "j2": _sb(24, "float32"), "r17": _sb(17, "float32"), "base": _sb(C, "int32"),
-    "dt1": _sb(64, "float32"), "d16s": _sb(16, "bfloat16"), "d4s": _sb(16, "bfloat16"),
+    "j16": _sb(72, "float32"), "j2": _sb(24, "float32"), "jx": _sb(24, "float32"), "r17": _sb(17, "float32"), "base": _sb(C, "int32"),
+    "dt1": _sb(64, "float32"), "dt2": _sb(32, "float32"), "ds": _sb(32, "bfloat16"),
     "d16": _sb(C, "bfloat16"), "d4": _sb(H, "bfloat16"),
     "offu": _sb(8, "uint16"), "offi": _sb(24, "uint16"), "offt": _sb(12, "uint16"), "offx": _sb(24, "uint16"), "offf": _sb(24, "uint16"),
     "lab": _sb(144, "int32"), "lt": _sb(216, "float32"), "jc": _sb(72, "float32"), "jb1": _sb(24, "float32"), "jb2": _sb(24, "float32"),
@@ -49,7 +49,7 @@ for _r in ("1", "2"):
         "z" + _r: _sb(4 * H, "bfloat16"), "t" + _r: _sb(4 * H, "bfloat16"), "vt" + _r: _sb(4 * H, "bfloat16"),
         "qz" + _r: _sb(H, X4), "sz" + _r: _sb(H, "uint8"),
     })
-NSEM = 140
+NSEM = 144
 SEMAPHORES = ["e%d" % k for k in range(NSEM)] + ["rq1", "rq2", "rl1", "rl2", "sent"]
 
 AL = AluOpType
@@ -128,6 +128,9 @@ def rank_program(g, core, T, topo):
             return op("A", lambda q: q.activation(out, in_, AF.Copy, scale=scale), deps)
         return op("A", lambda q: q.activation(out, in_, AF.Identity, bias=bias, scale=scale), deps)
 
+    def minus_sum(acc, out, in_, deps):
+        return op("A", lambda q: q.activation(out, in_, AF.Identity, scale=-1.0, accum_out=acc), deps)
+
     def mm(bank, w, sw, x, sx, m, deps=()):
         return op("P", lambda q: q.matmul_mx(T.ps[:, 512 * bank:512 * bank + m], w, sw, x, sx, True, True), deps)
 
@@ -164,70 +167,48 @@ def rank_program(g, core, T, topo):
     l_u = dma("A", T.us[:], T.u[:])
     l_l = []
     for e, t, o in (("A", T.li, 0), ("S", T.ri, 72)):
-        l_l.append(dma(e, T.lab[:, o:o + 24], t[:], [z_lab]))
-        l_l.append(dma(e, T.lab[16:128, o + 24:o + 48], t[0:112, :], [z_lab]))
+        l_l.append(dma(e, T.lab[16:128, o:o + 24], t[0:112, :], [z_lab]))
+        l_l.append(dma(e, T.lab[:, o + 24:o + 48], t[:], [z_lab]))
         l_l.append(dma(e, T.lab[0:112, o + 48:o + 72], t[16:128, :], [z_lab]))
     l_m = dma("S", T.ms[:], T.mid[:])
-    l_w = dma("S", T.qw[:].bitcast(dt.uint8), T.wc[:], [l_x1])
+    l_w = dma("S", T.qw[:].bitcast(dt.uint8), T.wc[:], [l_m])
     l_ws = dma("S", T.sw[:], T.ws[:])
-    l_v = dma("S", T.vs[:], T.v[:])
+    l_v = dma("S", T.vs[:], T.v[:], [l_w])
 
     g_p = iota(T.pcol[:], [[0, 1]], 0, 1, False)
-    g_j = iota(T.j16[:], [[0, 3], [16, 24]], 0, 0, True)
     g_r = iota(T.r17[:], [[1, 17]], -1, 0, True)
     g_i = iota(T.idm[:], [[1, 128]], 0, -1, True)
+    g_j = iota(T.j16[:], [[0, 3], [16, 24]], 0, 0, True)
+    g_x = iota(T.jx[:], [[2, 12], [24, 2]], 24, 0, True)
     g_j2 = iota(T.j2[:], [[1, 2], [32, 12]], 0, 0, True)
     g_b = iota(T.base[:], [[int(4 * AW), C]], 0, 0, False)
 
     z_e = fill(T.eb[:], 0.0)
-    z_f = [fill(T.fb1[:, C:C + 1], 0.0), None]
     c0 = ts(T.ci[:, 0:1], T.pcol[:], 15, None, AL.bitwise_and, None, [g_p])
     c1 = ts(T.ci[:, 1:2], T.pcol[:], 3, None, AL.bitwise_and)
     c2 = ts(T.ci[:, 2:3], T.pcol[:], 2, 3, AL.logical_shift_right, AL.bitwise_and)
     c3 = ts(T.ci[:, 3:4], T.pcol[:], 4, 1, AL.logical_shift_right, AL.bitwise_and)
-    k_u = cp(T.offu[:], T.j16[:, 0:8], [g_j])
+    z_f = [fill(T.fb1[:, C:C + 1], 0.0), None]
     k_c = cp(T.cf[:, 0:4], T.ci[:, 0:4], [c0, c1, c2, c3])
     ci_, ct_, cs_, ce_ = T.cf[:, 0:1], T.cf[:, 1:2], T.cf[:, 2:3], T.cf[:, 3:4]
-    nb_, t4_, i8_, jb1_, c4_, e25_, e47_, jb2_, fq_, lm_, la_ = [T.cd[:, k:k + 1] for k in range(11)]
+    nb_, t4_, i8_, jb1_, c4_, e23_, jb2_, fq_, lm_, la_ = [T.cd[:, k:k + 1] for k in range(10)]
     k_e = ts(T.eb[:, 3:515:4], T.idm[:], 0.0, None, AL.is_equal, None, [g_i, z_e])
-    a_e25 = act(e25_, ce_, 25.0, None, [k_c])
-    a_e47 = act(e47_, ce_, -47.0, 48.0)
+    a_e23 = act(e23_, ce_, -23.0, None, [k_c])
     a_i8 = act(i8_, ci_, 4 * AW)
-    k_nb = ts(nb_, ci_, 15.0, -B16, AL.is_lt, AL.mult, [k_c])
-    k_t4 = ts(t4_, cs_, 3.0, -B4, AL.is_lt, AL.mult)
-    k_a = ts(T.dt1[:, 0:16], T.r17[:, 1:17], ci_, -2 * B16, AL.is_equal, AL.mult, [g_r])
-    k_b = ts(T.dt1[:, 16:32], T.r17[:, 0:16], ci_, B16, AL.is_equal, AL.mult)
-    k_a4 = ts(T.dt1[:, 32:48], T.r17[:, 1:17], cs_, -2 * B4, AL.is_equal, AL.mult)
+    k_a = ts(T.dt1[:, 0:16], T.r17[:, 1:17], ci_, -2 * B16, AL.is_equal, AL.mult, [g_r, k_c])
+    k_a4 = ts(T.dt1[:, 16:32], T.r17[:, 1:17], cs_, -2 * B4, AL.is_equal, AL.mult)
+    k_b = ts(T.dt1[:, 32:48], T.r17[:, 0:16], ci_, B16, AL.is_equal, AL.mult)
     k_b4 = ts(T.dt1[:, 48:64], T.r17[:, 0:16], cs_, B4, AL.is_equal, AL.mult)
-    k_oi = ts(T.offi[:], T.j16[:, 0:24], 0.0, ci_, AL.mult, AL.add)
+    k_oi = ts(T.offi[:], T.j16[:, 0:24], 0.0, ci_, AL.mult, AL.add, [g_j])
+    k_d = tt(T.ds[:], T.dt1[:, 0:32], T.dt1[:, 32:64], AL.add, [k_a, k_b, k_a4, k_b4])
+    k_u = cp(T.offu[:], T.j16[:, 0:8])
     k_ot = ts(T.offt[:], T.j16[:, 0:12], 0.0, ct_, AL.mult, AL.add)
-    k_d16 = tt(T.d16s[:], T.dt1[:, 0:16], T.dt1[:, 16:32], AL.add, [k_a, k_b])
-    k_d4 = tt(T.d4s[:], T.dt1[:, 32:48], T.dt1[:, 48:64], AL.add, [k_a4, k_b4])
-    k_x0 = ts(T.offx[:, 0:24:2], T.j16[:, 0:12], 0.125, e25_, AL.mult, AL.add, [a_e25])
-    k_x1 = ts(T.offx[:, 1:24:2], T.j16[:, 0:12], 0.125, e47_, AL.mult, AL.add, [a_e47])
+    k_x = ts(T.offx[:], T.jx[:], e23_, None, AL.add, None, [a_e23, g_x])
     a_jc = act(T.jc[:], T.j16[:], 4 * AW, i8_, [a_i8, g_j])
-    a_jb = act(jb1_, nb_, -2.0, ci_, [k_nb])
-    a_c4 = act(c4_, ct_, AW, t4_, [k_t4])
-    a_jb1 = act(T.jb1[:], T.j16[:, 0:24], 1.0, jb1_, [a_jb])
-    a_d16 = act(T.d16[:], T.d16s[:].indirect(T.offi[:]), 1.0, None, [k_d16, k_oi])
-    a_d4 = act(T.d4[:], T.d4s[:].indirect(T.offt[:]), 1.0, None, [k_d4, k_ot])
-    q_e = [quant(T.qe[:, 128 * b:128 * b + 128], T.se[:, 128 * b:128 * b + 128], T.eb[:, 3 - b:515 - b], [k_e]) for b in range(4)]
+    a_d16 = act(T.d16[:], T.ds[:, 0:16].indirect(T.offi[:]), 1.0, None, [k_d, k_oi])
 
-    q_u = quant(T.qu[:], T.su[:], T.us[:], [l_u])
-    p_u = cp(T.qr[:].bitcast(dt.uint32), T.qu[:].bitcast(dt.uint32).indirect(T.offu[:]), [q_u, k_u])
-    p_us = act(T.sr[:], T.su[:].indirect(T.offu[:]), 1.0, None, [q_u, k_u])
-    v_1 = ts(T.lt[:, 0:72], T.lab[:, 72:144], 32.0, None, AL.mult, None, l_l[3:])
-    v_2 = tt(T.lt[:, 72:144], T.lab[:, 0:72], T.jc[:], AL.add, l_l[:3] + [a_jc])
-    q_x0 = quant(T.q1[:, 0:H], T.s1[:, 0:H], T.xs[:, 0:2 * C], [l_x0])
-    v_3 = tt(T.lt[:, 144:216], T.lt[:, 0:72], T.lt[:, 72:144], AL.add, [v_1, v_2])
-    q_x1 = quant(T.q1[:, H:C], T.s1[:, H:C], T.xs[:, 2 * C:4 * C], [l_x1])
-    a_x = act(T.xg[:], T.lt[:, 144:216].indirect(T.offx[:]), 1.0, None, [v_3, k_x0, k_x1])
-
-    def unpack(q, s, m, banks, deps):
-        return [mm(banks[b], T.qe[:, 128 * b:128 * b + 128], T.se[:, 128 * b:128 * b + 128], q, s, m, deps[b] + [q_e[b]]) for b in range(4)]
-
-    def evac(f, lo, m, banks, evs):
-        return [act(f[:, lo + b:lo + 4 * m:4], bank(banks[b], m), 0.5, None, [evs[b]]) for b in range(4)]
+    def q_eb(b):
+        return quant(T.qe[:, 128 * b:128 * b + 128], T.se[:, 128 * b:128 * b + 128], T.eb[:, 3 - b:515 - b], [k_e])
 
     def flags(r, b, lo, step, m, deps):
         fb = T["fb" + r]
@@ -235,9 +216,34 @@ def rank_program(g, core, T, topo):
         f2 = ts(fb[:, C + 1 + lo:2 * C + 1:step], fb[:, lo:C:step], (K + 1) / K, None, AL.mult, None, [f1])
         return [f1, f2]
 
-    def places(r, fl, jb, jdeps, val, vdeps):
+    q_e = [q_eb(0), q_eb(1)]
+    q_u = quant(T.qu[:], T.su[:], T.us[:], [l_u])
+    v_1 = ts(T.lt[:, 0:72], T.lab[:, 72:144], 32.0, None, AL.mult, None, l_l[3:])
+    v_2 = tt(T.lt[:, 72:144], T.lab[:, 0:72], T.jc[:], AL.add, l_l[:3] + [a_jc])
+    p_u = cp(T.qr[:].bitcast(dt.uint32), T.qu[:].bitcast(dt.uint32).indirect(T.offu[:]), [q_u, k_u])
+    p_us = act(T.sr[:], T.su[:].indirect(T.offu[:]), 1.0, None, [q_u, k_u])
+    v_3 = tt(T.lt[:, 144:216], T.lt[:, 0:72], T.lt[:, 72:144], AL.add, [v_1, v_2])
+    a_x = act(T.xg[:], T.lt[:, 144:216].indirect(T.offx[:]), 1.0, None, [v_3, k_x])
+    a_nb = minus_sum(nb_, T.dt2[:, 0:16], T.dt1[:, 32:48], [k_b])
+    a_t4 = minus_sum(t4_, T.dt2[:, 16:20], T.dt1[:, 48:52], [k_b4])
+    a_jb = act(jb1_, nb_, -2.0, ci_, [a_nb])
+    a_c4 = act(c4_, ct_, AW, t4_, [a_t4])
+    a_jb1 = act(T.jb1[:], T.j16[:, 0:24], 1.0, jb1_, [a_jb])
+    q_x0 = quant(T.q1[:, 0:H], T.s1[:, 0:H], T.xs[:, 0:2 * C], [l_x0])
+    q_x1 = quant(T.q1[:, H:C], T.s1[:, H:C], T.xs[:, 2 * C:4 * C], [l_x1])
+    m_s = mm(0, T.qr[:], T.sr[:], T.q1[:], T.s1[:], C, [p_u, p_us, q_x0, q_x1])
+    q_e += [q_eb(2), q_eb(3)]
+
+    def unpack(q, s, m, banks, deps):
+        return [mm(banks[b], T.qe[:, 128 * b:128 * b + 128], T.se[:, 128 * b:128 * b + 128], q, s, m, deps[b] + [q_e[b]]) for b in range(4)]
+
+    def evac(f, lo, m, banks, evs):
+        return [act(f[:, lo + b:lo + 4 * m:4], bank(banks[b], m), 0.5, None, [evs[b]]) for b in range(4)]
+
+    def places(r, fl, jb, jdeps, extra, val):
         fb, ys, yh, sm = T["fb" + r], T["ys" + r], T["yh" + r], T["sm" + r]
         s = scan(ys[:, 0:C + 1], fb[:, C:2 * C + 1], fb[:, 0:C + 1], K, AL.add, AL.subtract, fl)
+        vdeps = extra(0)
         tc = cp(sm[:, 72:73], ys[:, C:C + 1], [s])
         if r == "1":
             hs = [scan(yh[:], T.d16[:], ys[:, 0:C], 0.0, AL.add, AL.max, [s, a_d16])]
@@ -246,27 +252,30 @@ def rank_program(g, core, T, topo):
         jt = ts(sm[:, 0:24], jb, sm[:, 72:73], None, AL.add, None, [tc] + jdeps)
         d = tt(sm[:, 24:48], sm[:, 0:24], yh[:, 15:C:16], AL.subtract, [jt] + hs)
         mn = tt(sm[:, 48:72], sm[:, 24:48], yh[:, 15:C:16], AL.min, [d])
-        po = ts(T["pos" + r][:], sm[:, 48:72], nb_, None, AL.add, None, [mn, k_nb])
+        po = ts(T["pos" + r][:], sm[:, 48:72], nb_, None, AL.add, None, [mn, a_nb])
+        vdeps = vdeps + extra(1)
         return cp(T["w" + r][:].indirect(T["pos" + r][:]), val, [po] + vdeps)
 
-    def layer(r, sc, fdeps, mdeps, bdeps, between, gap, q, s):
+    def layer(r, sc, fdeps, mdeps, bdeps, between, early, gap, q, s):
         w, hw, im, fm = T["w" + r], T["hw" + r], T["im" + r], T["fm" + r]
         ol, oh, om = T["ol" + r], T["oh" + r], T["om" + r]
         f, fh, p, pp, z, t, vt = [T[x + r] for x in ("f", "fh", "p", "pp", "z", "t", "vt")]
         sh = scan(hw[:, H:C], T.d4[:], w[:, 1:C:2], 0.0, AL.add, AL.max, [sc, a_d4])
-        sl = scan(hw[:, 0:H], T.d4[:], w[:, 0:C:2], 0.0, AL.add, AL.max, [sc])
+        early(0)
         oh_ = ts(oh[:], hw[:, H + 3:C:4], c4_, 1.0 / AW, AL.add, AL.mult, [sh, a_c4])
         gh = [act(fh[:, C * k:C * k + C], f[:].indirect(oh[:, 24 * k:24 * k + 24]), 1.0, None, [oh_] + fdeps) for k in range(2)]
         between()
+        sl = scan(hw[:, 0:H], T.d4[:], w[:, 0:C:2], 0.0, AL.add, AL.max, [sc])
+        early(1)
         i0 = cp(im[:, 0:96], hw[:, 3:C:4], [sh, sl])
         ol_ = ts(ol[:], hw[:, 3:H:4], c4_, 1.0 / AW, AL.add, AL.mult, [sl])
         i1 = ts(im[:, 96:144], im[:, 0:48], 31 * 32, None, AL.bitwise_and, None, [i0])
         i2 = ts(im[:, 144:192], im[:, 48:96], 31, None, AL.bitwise_and, None, [i0])
         i3 = ts(fm[:, 0:48], im[:, 96:144], I / 32.0, None, AL.mult, None, [i1])
+        mx = [tt(p[:, 0:C], f[:].indirect(ol[:, 0:24]), fh[:, 0:C], AL.max, [ol_, gh[0]] + fdeps)]
         i4 = tt(fm[:, 48:96], fm[:, 0:48], im[:, 144:192], AL.add, [i3, i2])
+        mx.append(tt(p[:, C:2 * C], f[:].indirect(ol[:, 24:48]), fh[:, C:2 * C], AL.max, [ol_, gh[1]]))
         om_ = ts(om[:], fm[:, 48:96], 4.0, ct_, AL.mult, AL.add, [i4])
-        mx = [tt(p[:, C * k:C * k + C], f[:].indirect(ol[:, 24 * k:24 * k + 24]), fh[:, C * k:C * k + C], AL.max, [ol_, gh[k]] + fdeps)
-              for k in range(2)]
         a_p = act(pp[:], p[:], 64.0, None, mx)
         zz = tt(z[:], T.mf[:].indirect(om[:]), p[:], AL.add, mx + [om_] + mdeps())
         qz = quant(T["qz" + r][:], T["sz" + r][:], z[:], [zz])
@@ -278,26 +287,35 @@ def rank_program(g, core, T, topo):
         sv.append(ts(vt[:, 3:4 * H:4], t[:, 3:4 * H:4], 0.03125, None, AL.mult, None, [ad[3]]))
         return quant(q, s, vt[:], sv), ad
 
-    m_s = mm(0, T.qr[:], T.sr[:], T.q1[:], T.s1[:], C, [p_u, p_us, q_x0, q_x1])
+    keep = {}
+    mb = [5, 6, 7, 0]
+    a_d4 = act(T.d4[:], T.ds[:, 16:32].indirect(T.offt[:]), 1.0, None, [k_d, k_ot])
     m_d = unpack(T.q1[:], T.s1[:], C, [1, 2, 3, 4], [[]] * 4)
-    q_m = quant(T.qm[:], T.sm[:], T.ms[:], [l_m])
     fl = flags("1", 0, 0, 1, C, [m_s])
     e_f = evac(T.f1, 0, C, [1, 2, 3, 4], m_d)
-    m_m = unpack(T.qm[:], T.sm[:], NM, [5, 6, 7, 0], [[q_m]] * 3 + [[fl[0]]])
-    tr = op("V", lambda q: q.transpose(T.val1[:], T.xg[:]), [a_x])
-    e_m = [act(T.mf[:, b:4 * NM:4], bank([5, 6, 7, 0][b], NM), 0.5, None, [m_m[b]]) for b in range(2)]
-    sc = places("1", fl + [z_f[0]], T.jb1[:], [a_jb1], T.val1[:], [tr])
+    e_m = []
+
+    def extra1(k):
+        if k == 0:
+            return [op("V", lambda q: q.transpose(T.val1[:], T.xg[:]), [a_x])]
+        q_m = quant(T.qm[:], T.sm[:], T.ms[:], [l_m])
+        keep["mm"] = unpack(T.qm[:], T.sm[:], NM, mb, [[q_m], [], [], [fl[0]]])
+        for b in range(2):
+            e_m.append(act(T.mf[:, b:4 * NM:4], bank(mb[b], NM), 0.5, None, [keep["mm"][b]]))
+        return []
+
+    sc = places("1", fl + [z_f[0]], T.jb1[:], [a_jb1], extra1, T.val1[:])
 
     def between1():
         for b in (2, 3):
-            e_m.append(act(T.mf[:, b:4 * NM:4], bank([5, 6, 7, 0][b], NM), 0.5, None, [m_m[b]]))
+            e_m.append(act(T.mf[:, b:4 * NM:4], bank(mb[b], NM), 0.5, None, [keep["mm"][b]]))
 
-    keep = {}
-
-    def gap1():
-        i0 = cp(T.iw[:], T.w1[:], [sc])
-        keep["xa"] = ts(T.xa[:], T.iw[:, 0:C:2], 31, None, AL.bitwise_and, None, [i0])
-        keep["xb"] = ts(T.xb[:], T.iw[:, 1:C:2], 31 * 32, None, AL.bitwise_and, None, [i0])
+    def early1(k):
+        if k == 0:
+            keep["iw"] = cp(T.iw[:], T.w1[:], [sc])
+            return
+        keep["xa"] = ts(T.xa[:], T.iw[:, 0:C:2], 31, None, AL.bitwise_and, None, [keep["iw"]])
+        keep["xb"] = ts(T.xb[:], T.iw[:, 1:C:2], 31 * 32, None, AL.bitwise_and)
         for d in (keep["xa"], keep["xb"], g_b):
             wait("G", d)
         rid, pid, _e = topo.addr(dst[0])
@@ -306,19 +324,20 @@ def rank_program(g, core, T, topo):
                            local_sem=T.sem["sent"])
         sent[0] += width(core)
 
-    q_v1, ad1 = layer("1", sc, e_f, lambda: e_m, e_f, between1, gap1, T.q2[:, H:C], T.s2[:, H:C])
+    def gap1():
+        keep["o1"] = tt(T.xc[:], T.xa[:], T.xb[:], AL.add, [keep["xa"], keep["xb"]])
+
+    q_v1, ad1 = layer("1", sc, e_f, lambda: e_m, e_f, between1, early1, gap1, T.q2[:, H:C], T.s2[:, H:C])
     push(0, T.q2[:, 0:H].bitcast(dt.uint8), T.q2[:, H:C].bitcast(dt.uint8), "rq1", [q_v1])
     push(0, T.s2[:, 0:H], T.s2[:, H:C], "rq1", [q_v1])
 
     m_so = mm(5, T.qr[:], T.sr[:], T.q2[:, H:C], T.s2[:, H:C], H, [q_v1, e_m[0]])
     m_do = unpack(T.q2[:, H:C], T.s2[:, H:C], H, [1, 2, 3, 4], [[]] * 4)
     z_f[1] = fill(T.fb2[:, C:C + 1], 0.0)
-    k_jb = ts(jb2_, ci_, nb_, 2.0, AL.subtract, AL.mult, [k_nb])
-    o_1 = tt(T.xc[:], T.xa[:], T.xb[:], AL.add, [keep["xa"], keep["xb"]])
+    k_jb = ts(jb2_, ci_, nb_, 2.0, AL.subtract, AL.mult, [a_nb])
+    o_2 = tt(T.val2[:, H:C], T.xc[:], T.base[:, H:C], AL.add, [keep["o1"], g_b])
     flo = flags("2", 5, 1, 2, H, [m_so])
     k_jb2 = ts(T.jb2[:], T.j2[:], jb2_, None, AL.add, None, [k_jb, g_j2])
-    o_2 = tt(T.val2[:, H:C], T.xc[:], T.base[:, H:C], AL.add, [o_1, g_b])
-    q_v = quant(T.qv[:], T.sv[:], T.vs[:], [l_v])
     e_o = evac(T.f2, 4 * H, H, [1, 2, 3, 4], m_do)
 
     r1 = ("rq1", 2 * width(src[0]))
@@ -326,19 +345,25 @@ def rank_program(g, core, T, topo):
     m_da = unpack(T.q2[:, 0:H], T.s2[:, 0:H], H, [1, 2, 3, 4], [[e] for e in e_o])
     fla = flags("2", 6, 0, 2, H, [m_sa])
     e_a = evac(T.f2, 0, H, [1, 2, 3, 4], m_da)
-    sc2 = places("2", fla + flo + [z_f[1]], T.jb2[:], [k_jb2], T.val2[:], [o_2, ("rl1", width(src[0]))])
+    sc2 = places("2", fla + flo + [z_f[1]], T.jb2[:], [k_jb2], lambda k: [[], [o_2, ("rl1", width(src[0]))]][k], T.val2[:])
 
     def between2():
-        a0 = act(T.wd[:, 0:H], T.w2[:, 0:C:2], 1.0, None, [sc2])
         a1 = act(T.wd[:, H:C], T.w2[:, 1:C:2], 1.0, None, [sc2])
-        keep["lw"] = dma("S", T.lw[:], T.wd[0:128:16, :], [a0, a1])
+        keep["lw"] = dma("S", T.lw[:], T.wd[0:128:16, :], [keep["a0"], a1])
         push(1, T.lwr[:], T.lw[:], "rl2", [keep["lw"]])
 
-    q_v2, ad2 = layer("2", sc2, e_o + e_a, lambda: [], e_a, between2, lambda: None, T.q3[:, H:C], T.s3[:, H:C])
+    def early2(k):
+        if k == 0:
+            keep["a0"] = act(T.wd[:, 0:H], T.w2[:, 0:C:2], 1.0, None, [sc2])
+
+    def gap2():
+        keep["qv"] = quant(T.qv[:], T.sv[:], T.vs[:], [l_v])
+
+    q_v2, ad2 = layer("2", sc2, e_o + e_a, lambda: [], e_a, between2, early2, gap2, T.q3[:, H:C], T.s3[:, H:C])
     push(1, T.q3[:, 0:H].bitcast(dt.uint8), T.q3[:, H:C].bitcast(dt.uint8), "rq2", [q_v2])
     push(1, T.s3[:, 0:H], T.s3[:, H:C], "rq2", [q_v2])
 
-    m_yo = mm(5, T.qv[:], T.sv[:], T.q3[:, H:C], T.s3[:, H:C], H, [q_v2, q_v, flo[0]])
+    m_yo = mm(5, T.qv[:], T.sv[:], T.q3[:, H:C], T.s3[:, H:C], H, [q_v2, keep["qv"], flo[0]])
     c4 = ts(T.ci[:, 4:5], T.pcol[:], 3, 1, AL.logical_shift_right, AL.bitwise_and)
     c5 = ts(T.ci[:, 5:6], T.pcol[:], 1, None, AL.bitwise_and)
     c6 = ts(T.ci[:, 6:7], T.pcol[:], 1, 7, AL.logical_shift_right, AL.bitwise_and)
@@ -356,13 +381,12 @@ def rank_program(g, core, T, topo):
 
     r2 = ("rq2", 2 * width(src[1]))
     m_ya = mm(6, T.qv[:], T.sv[:], T.q3[:, 0:H], T.s3[:, 0:H], H, [r2, fla[0]])
-    p_c = cp(T.qo[:].bitcast(dt.uint32), T.q3[:].bitcast(dt.uint32).indirect(T.offf[:]), [r2, q_v2, k_of])
-    y_a = act(T.yb[:, 0:C:2], bank(6, H), 1.0, None, [m_ya])
-    dma("S", T.y[:], T.yb[:], [y_a, y_o])
     p_s = act(T.so[:], T.s3[:].indirect(T.offf[:]), 1.0, None, [r2, q_v2, k_of])
+    p_c = cp(T.qo[:].bitcast(dt.uint32), T.q3[:].bitcast(dt.uint32).indirect(T.offf[:]), [r2, q_v2, k_of])
     dma("S", T.oc[:], T.qo[:].bitcast(dt.uint8), [p_c])
+    dma("S", T.y[:], T.yb[:], [cp(T.yb[:, 0:C:2], bank(6, H), [m_ya]), y_o])
     for k in range(4):
-        dma("A" if k % 2 == 0 else "S", T.osc[4 * k:4 * k + 4, :], T.so[32 * k:32 * k + 4, :], [p_s])
+        dma("A" if k < 3 else "S", T.osc[4 * k:4 * k + 4, :], T.so[32 * k:32 * k + 4, :], [p_s])
 
     wait("G", ("sent", sent[0]))
     for name in order:

@@ -1,16 +1,18 @@
 from concourse.bass import DstId, RemoteDMATransfer
-from concourse.mybir import dt, AluOpType, ActivationFunctionType
+from concourse.mybir import dt, AluOpType, ActivationFunctionType, AxisListType
 
 C = 384
 H = C // 2
+NA = 128
 NM = 400
-I = 20
 HALF = "float16"
 X4 = "float8_e4m3fn_x4"
 K = 512.0
 B16 = 1024.0
-B4 = 4194304.0
+L4 = 4194304.0
+L1 = 1024.0
 AW = 2048.0
+S = 4 * AW
 
 
 def _sb(n, d):
@@ -25,31 +27,35 @@ SCRATCH = {
     "qu": _sb(128, X4), "su": _sb(128, "uint8"), "qr": _sb(128, X4), "sr": _sb(128, "uint8"),
     "qv": _sb(128, X4), "sv": _sb(128, "uint8"), "qm": _sb(NM, X4), "sm": _sb(NM, "uint8"),
     "qw": _sb(512, X4), "sw": _sb(512, "uint8"), "qe": _sb(512, X4), "se": _sb(512, "uint8"),
-    "eb": _sb(520, "bfloat16"), "idm": _sb(128, "float32"),
-    "pcol": _sb(1, "int32"), "ci": _sb(8, "int32"), "cf": _sb(8, "float32"), "cd": _sb(16, "float32"),
-    "j16": _sb(72, "float32"), "j2": _sb(24, "float32"), "jx": _sb(24, "float32"), "r17": _sb(17, "float32"), "base": _sb(C, "int32"),
-    "dt1": _sb(64, "float32"), "dt2": _sb(32, "float32"), "ds": _sb(32, "bfloat16"),
-    "d16": _sb(C, "bfloat16"), "d4": _sb(H, "bfloat16"),
-    "offu": _sb(8, "uint16"), "offi": _sb(24, "uint16"), "offt": _sb(12, "uint16"), "offx": _sb(24, "uint16"), "offf": _sb(24, "uint16"),
-    "lab": _sb(144, "int32"), "lt": _sb(216, "float32"), "jc": _sb(72, "float32"), "jb1": _sb(24, "float32"), "jb2": _sb(24, "float32"),
-    "xg": _sb(C, "float32"), "val1": _sb(C, "float32"), "val2": _sb(C, "int32"),
+    "eb": _sb(520, "bfloat16"),
+    "ia": _sb(64, "int32"), "ib": _sb(64, "int32"), "ic": _sb(64, "int32"), "ea": _sb(64, "int32"), "ec": _sb(66, "int32"),
+    "ed": _sb(64, "int32"), "ee": _sb(128, "int32"),
+    "ds": _sb(128, "bfloat16"), "dm": _sb(64, "bfloat16"), "dn": _sb(64, "bfloat16"), "dp": _sb(128, "bfloat16"),
+    "cf": _sb(4, "float32"), "cd": _sb(24, "float32"),
+    "jq": _sb(48, "float32"), "j2": _sb(24, "float32"), "five": _sb(96, "float32"), "jm": _sb(24, "float32"),
+    "d16": _sb(C, "bfloat16"), "d4": _sb(H, "bfloat16"), "d4t": _sb(48, "bfloat16"), "d16s": _sb(H, "bfloat16"),
+    "offs": _sb(32, "uint16"), "offf": _sb(24, "uint16"),
+    "lab": _sb(48, "int32"), "lt": _sb(48, "float32"), "jc": _sb(24, "float32"), "jb1": _sb(24, "float32"), "jb2": _sb(48, "float32"),
     "mf": _sb(4 * NM, "bfloat16"),
-    "iw": _sb(C, "int32"), "xa": _sb(H, "int32"), "xb": _sb(H, "int32"), "xc": _sb(H, "int32"),
+    "fb": _sb(2 * C + 2, HALF), "ys": _sb(C, HALF),
+    "xa": _sb(96, "int32"), "xb": _sb(96, "float32"), "xc": _sb(12, "float32"), "xd": _sb(12, "float32"),
     "wd": _sb(C, "float32"), "lw": _sb(24, "float32"), "lwr": _sb(24, "float32"),
     "lri": _sb(48, "int32"), "lrj": _sb(48, "int32"), "lrf": _sb(48, "float32"),
     "yb": _sb(C, "float32"),
 }
 for _r in ("1", "2"):
     SCRATCH.update({
-        "f" + _r: _sb(4 * C, "bfloat16"), "fb" + _r: _sb(2 * C + 2, HALF), "ys" + _r: _sb(C + 2, HALF), "yh" + _r: _sb(C, HALF),
-        "sm" + _r: _sb(80, "float32"), "pos" + _r: _sb(24, "uint16"), "w" + _r: _sb(C, "float32"), "hw" + _r: _sb(C, "float32"),
+        "ta" + _r: _sb(96, "float32"), "tb" + _r: _sb(96, "float32"), "tc" + _r: _sb(64, "float32"),
+        "xg" + _r: _sb(C, "float32"), "val" + _r: _sb(C, "float32"), "w" + _r: _sb(C, "float32"),
+        "f" + _r: _sb(4 * C, "bfloat16"), "yh" + _r: _sb(C, HALF),
+        "sm" + _r: _sb(80, "float32"), "pos" + _r: _sb(24, "uint16"), "hw" + _r: _sb(C, "int32"),
         "ol" + _r: _sb(48, "uint16"), "oh" + _r: _sb(48, "uint16"), "om" + _r: _sb(48, "uint16"),
-        "im" + _r: _sb(192, "int32"), "fm" + _r: _sb(96, "float32"),
+        "im" + _r: _sb(96, "int32"), "fm" + _r: _sb(96, "float32"),
         "fh" + _r: _sb(4 * H, "bfloat16"), "p" + _r: _sb(4 * H, "bfloat16"), "pp" + _r: _sb(4 * H, "bfloat16"),
         "z" + _r: _sb(4 * H, "bfloat16"), "t" + _r: _sb(4 * H, "bfloat16"), "vt" + _r: _sb(4 * H, "bfloat16"),
-        "qz" + _r: _sb(H, X4), "sz" + _r: _sb(H, "uint8"),
+        "qz" + _r: _sb(256, X4), "sz" + _r: _sb(256, "uint8"),
     })
-NSEM = 144
+NSEM = 140
 SEMAPHORES = ["e%d" % k for k in range(NSEM)] + ["rq1", "rq2", "rl1", "rl2", "sent"]
 
 AL = AluOpType
@@ -62,44 +68,14 @@ def rank_program(g, core, T, topo):
         return
     n = len(T.cores)
     queues = {"V": g.vector, "A": g.scalar, "P": g.tensor, "S": g.sync, "G": g}
-    waited = {k: {} for k in queues}
-    pool = {k: [] for k in queues}
-    count = {}
-    order = []
+    calls = []
 
-    def wait(e, ev):
-        if waited[e].get(ev[0], 0) < ev[1]:
-            queues[e].wait_ge(T.sem[ev[0]], ev[1])
-            waited[e][ev[0]] = ev[1]
-
-    def fresh():
-        name = "e%d" % len(order)
-        order.append(name)
-        count[name] = 0
-        return name
-
-    def op(e, call, deps=()):
-        for d in deps:
-            wait(e, d)
-        name = None
-        for s in pool[e]:
-            if waited[e].get(s, 0) >= count[s]:
-                name = s
-                break
-        if name is None:
-            name = fresh()
-            pool[e].append(name)
-        call(queues[e]).then_inc(T.sem[name], 1)
-        count[name] += 1
-        return (name, count[name])
+    def op(e, call, deps=(), inc=1):
+        calls.append((e, call, [d for d in deps if d is not None], inc))
+        return len(calls) - 1
 
     def dma(e, out, in_, deps=()):
-        for d in deps:
-            wait(e, d)
-        name = fresh()
-        queues[e].dma_start(out, in_).then_inc(T.sem[name], 16)
-        count[name] = 16
-        return (name, 16)
+        return op(e, lambda q: q.dma_start(out, in_), deps, 16)
 
     def ts(out, in0, a, b, o0, o1=None, deps=()):
         if o1 is None:
@@ -112,6 +88,12 @@ def rank_program(g, core, T, topo):
     def cp(out, in_, deps=()):
         return op("V", lambda q: q.tensor_copy(out, in_), deps)
 
+    def turn(out, in_, deps=()):
+        return op("V", lambda q: q.transpose(out, in_), deps)
+
+    def total(out, in_, deps=()):
+        return op("V", lambda q: q.tensor_reduce(out, in_, AxisListType.X, AL.add), deps)
+
     def scan(out, d0, d1, init, o0, o1, deps=()):
         return op("V", lambda q: q.tensor_tensor_scan(out, d0, d1, init, o0, o1), deps)
 
@@ -121,26 +103,23 @@ def rank_program(g, core, T, topo):
     def fill(ap, c):
         return op("V", lambda q: q.memset(ap, c))
 
-    def act(out, in_, scale=1.0, bias=None, deps=()):
+    def act(out, in_, scale=1.0, bias=None, deps=(), func=None):
         if bias is None:
             if isinstance(scale, float) and scale == 1.0:
                 return op("A", lambda q: q.activation(out, in_, AF.Copy), deps)
             return op("A", lambda q: q.activation(out, in_, AF.Copy, scale=scale), deps)
-        return op("A", lambda q: q.activation(out, in_, AF.Identity, bias=bias, scale=scale), deps)
+        return op("A", lambda q: q.activation(out, in_, func or AF.Identity, bias=bias, scale=scale), deps)
 
-    def minus_sum(acc, out, in_, deps):
-        return op("A", lambda q: q.activation(out, in_, AF.Identity, scale=-1.0, accum_out=acc), deps)
-
-    def mm(bank, w, sw, x, sx, m, deps=()):
-        return op("P", lambda q: q.matmul_mx(T.ps[:, 512 * bank:512 * bank + m], w, sw, x, sx, True, True), deps)
+    def mm(b, w, sw, x, sx, m, deps=()):
+        return op("P", lambda q: q.matmul_mx(T.ps[:, 512 * b:512 * b + m], w, sw, x, sx, True, True), deps)
 
     def iota(out, pattern, base, cm, flt):
         if flt:
             return op("G", lambda q: q.iota(out, pattern, base, cm, allow_small_or_imprecise_dtypes=True))
         return op("G", lambda q: q.iota(out, pattern, base, cm))
 
-    def bank(b, m):
-        return T.ps[:, 512 * b:512 * b + m]
+    def bank(b, lo, hi):
+        return T.ps[:, 512 * b + lo:512 * b + hi]
 
     dst = [T.cores[(rank + 1) % n], T.cores[(rank + 2) % n]]
     src = [T.cores[(rank - 1) % n], T.cores[(rank - 2) % n]]
@@ -155,240 +134,318 @@ def rank_program(g, core, T, topo):
     sent = [0]
 
     def push(k, out, in_, sem, deps):
-        for d in deps:
-            wait("G", d)
         rid, pid, _e = topo.addr(dst[k])
-        g.remote_dma(out, in_, T.sem[sem], T.sem["sent"], pid, rid, lanes(core))
+        op("G", lambda q: q.remote_dma(out, in_, T.sem[sem], T.sem["sent"], pid, rid, lanes(core)), deps, 0)
         sent[0] += width(core)
 
-    z_lab = fill(T.lab[:], 0)
-    l_x0 = dma("S", T.xs[:, 0:2 * C], T.x[:, 0:2 * C])
-    l_x1 = dma("S", T.xs[:, 2 * C:4 * C], T.x[:, 2 * C:4 * C])
-    l_u = dma("A", T.us[:], T.u[:])
-    l_l = []
-    for e, t, o in (("A", T.li, 0), ("S", T.ri, 72)):
-        l_l.append(dma(e, T.lab[16:128, o:o + 24], t[0:112, :], [z_lab]))
-        l_l.append(dma(e, T.lab[:, o + 24:o + 48], t[:], [z_lab]))
-        l_l.append(dma(e, T.lab[0:112, o + 48:o + 72], t[16:128, :], [z_lab]))
-    l_m = dma("S", T.ms[:], T.mid[:])
-    l_w = dma("S", T.qw[:].bitcast(dt.uint8), T.wc[:], [l_m])
+    l_u = dma("S", T.us[:], T.u[:])
+    l_x = dma("S", T.xs[:], T.x[:])
+    l_r = dma("A", T.lab[:, 24:48], T.ri[:])
+    l_l = dma("A", T.lab[:, 0:24], T.li[:])
+    cut = [0, NM // 2, NM]
+    l_m = [dma("S", T.ms[:, 4 * cut[k]:4 * cut[k + 1]], T.mid[:, 4 * cut[k]:4 * cut[k + 1]], [l_u]) for k in range(2)]
+    l_w = dma("S", T.qw[:].bitcast(dt.uint8), T.wc[:], [l_m[0]])
     l_ws = dma("S", T.sw[:], T.ws[:])
-    l_v = dma("S", T.vs[:], T.v[:], [l_w])
-
-    g_p = iota(T.pcol[:], [[0, 1]], 0, 1, False)
-    g_r = iota(T.r17[:], [[1, 17]], -1, 0, True)
-    g_i = iota(T.idm[:], [[1, 128]], 0, -1, True)
-    g_j = iota(T.j16[:], [[0, 3], [16, 24]], 0, 0, True)
-    g_x = iota(T.jx[:], [[2, 12], [24, 2]], 24, 0, True)
-    g_j2 = iota(T.j2[:], [[1, 2], [32, 12]], 0, 0, True)
-    g_b = iota(T.base[:], [[int(4 * AW), C]], 0, 0, False)
 
     z_e = fill(T.eb[:], 0.0)
-    c0 = ts(T.ci[:, 0:1], T.pcol[:], 15, None, AL.bitwise_and, None, [g_p])
-    c1 = ts(T.ci[:, 1:2], T.pcol[:], 3, None, AL.bitwise_and)
-    c2 = ts(T.ci[:, 2:3], T.pcol[:], 2, 3, AL.logical_shift_right, AL.bitwise_and)
-    c3 = ts(T.ci[:, 3:4], T.pcol[:], 4, 1, AL.logical_shift_right, AL.bitwise_and)
-    z_f = [fill(T.fb1[:, C:C + 1], 0.0), None]
-    k_c = cp(T.cf[:, 0:4], T.ci[:, 0:4], [c0, c1, c2, c3])
-    ci_, ct_, cs_, ce_ = T.cf[:, 0:1], T.cf[:, 1:2], T.cf[:, 2:3], T.cf[:, 3:4]
-    nb_, t4_, i8_, jb1_, c4_, e23_, jb2_, fq_, lm_, la_ = [T.cd[:, k:k + 1] for k in range(10)]
-    k_e = ts(T.eb[:, 3:515:4], T.idm[:], 0.0, None, AL.is_equal, None, [g_i, z_e])
-    a_e23 = act(e23_, ce_, -23.0, None, [k_c])
-    a_i8 = act(i8_, ci_, 4 * AW)
-    k_a = ts(T.dt1[:, 0:16], T.r17[:, 1:17], ci_, -2 * B16, AL.is_equal, AL.mult, [g_r, k_c])
-    k_a4 = ts(T.dt1[:, 16:32], T.r17[:, 1:17], cs_, -2 * B4, AL.is_equal, AL.mult)
-    k_b = ts(T.dt1[:, 32:48], T.r17[:, 0:16], ci_, B16, AL.is_equal, AL.mult)
-    k_b4 = ts(T.dt1[:, 48:64], T.r17[:, 0:16], cs_, B4, AL.is_equal, AL.mult)
-    k_oi = ts(T.offi[:], T.j16[:, 0:24], 0.0, ci_, AL.mult, AL.add, [g_j])
-    k_d = tt(T.ds[:], T.dt1[:, 0:32], T.dt1[:, 32:64], AL.add, [k_a, k_b, k_a4, k_b4])
-    k_u = cp(T.offu[:], T.j16[:, 0:8])
-    k_ot = ts(T.offt[:], T.j16[:, 0:12], 0.0, ct_, AL.mult, AL.add)
-    k_x = ts(T.offx[:], T.jx[:], e23_, None, AL.add, None, [a_e23, g_x])
-    a_jc = act(T.jc[:], T.j16[:], 4 * AW, i8_, [a_i8, g_j])
-    a_d16 = act(T.d16[:], T.ds[:, 0:16].indirect(T.offi[:]), 1.0, None, [k_d, k_oi])
+    g_a = iota(T.ia[:], [[-1, 64]], 64, 1, False)
+    g_b = iota(T.ib[:], [[-4, 64]], 256, 1, False)
+    g_j = iota(T.jq[:, 24:48], [[16, 24]], 0, 0, True)
+    g_x = iota(T.jq[:, 0:24], [[1, 12], [-32, 2]], 32, 0, True)
+    g_e = op("G", lambda q: q.affine_select(T.eb[:, 3:515:4], T.eb[:, 3:515:4], [[1, 128]], AL.not_equal, 1.0, 0, -1), [z_e])
+    g_j2 = iota(T.j2[:], [[1, 2], [32, 12]], 0, 0, True)
+    g_5 = iota(T.five[:], [[0, 48], [5, 2]], 0, 0, True)
+    g_c = iota(T.ic[:], [[-1, 64]], 64, 0, False)
+    j16, offx, offu = T.jq[:, 24:48], T.offs[:, 0:24], T.offs[:, 24:32]
+    ci_, cs_, co_ = T.cf[:, 0:1], T.cf[:, 2:3], T.cf[:, 3:4]
+    mu_, nb_, is_, k0_, k1_, k2_, ct_, c3_, c4_, lm_, ih_, fq_, sg_, b0_, b1_ = [T.cd[:, k:k + 1] for k in range(15)]
+    keep = {}
 
     def q_eb(b):
-        return quant(T.qe[:, 128 * b:128 * b + 128], T.se[:, 128 * b:128 * b + 128], T.eb[:, 3 - b:515 - b], [k_e])
+        return quant(T.qe[:, 128 * b:128 * b + 128], T.se[:, 128 * b:128 * b + 128], T.eb[:, 3 - b:515 - b], [g_e])
 
-    def flags(r, b, lo, step, m, deps):
-        fb = T["fb" + r]
-        f1 = ts(fb[:, lo:C:step], bank(b, m), 0.0, K, AL.is_gt, AL.mult, deps)
-        f2 = ts(fb[:, C + 1 + lo:2 * C + 1:step], fb[:, lo:C:step], (K + 1) / K, None, AL.mult, None, [f1])
-        return [f1, f2]
+    def square(d, deps):
+        return act(d[:, 64:128], d[:, 0:64], 1.0, -130.5, deps, AF.Square)
 
-    q_e = [q_eb(0), q_eb(1)]
+    def steps(out, d, m, sq):
+        return [act(out[:, 64 * k:64 * k + 64], d[:, 64:128], -B16 / 2, 2.25 * B16 / 2, [sq]) for k in range(m // 64)]
+
+    def spread_a(r, deps):
+        return turn(T["tb" + r][:], T["ta" + r][:], deps)
+
+    def spread_b(r, dep):
+        tb = T["tb" + r]
+        return [cp(tb[:, 32:48], tb[:, 80:96], [dep]), cp(tb[:, 48:64], tb[:, 0:16], [dep])]
+
+    def spread_c(r, deps):
+        return turn(T["tc" + r][:], T["tb" + r][:, 16:80], deps)
+
+    z_t = [fill(T.ta1[:], 0.0), fill(T.ta2[:], 0.0)]
+    z_f = fill(T.fb[:, C:C + 1], 0.0)
+    c_a = ts(T.ea[:], T.ia[:], 15, None, AL.bitwise_and, None, [g_a])
+    c_o = ts(T.ec[:, 64:65], T.ia[:, 0:1], 1, None, AL.bitwise_and)
+    c_t = ts(T.ed[:, 0:48], T.ia[:, 0:48], 3, None, AL.bitwise_and)
+    c_d = ts(T.ds[:, 0:64], T.ea[:], 0.0695, 128.465, AL.mult, AL.add, [c_a])
+    c_b = ts(T.ec[:, 0:64], T.ib[:], 2, 3, AL.logical_shift_right, AL.bitwise_and, [g_b])
+    c_c = cp(ci_, T.ea[:, 0:1], [c_a])
+    c_n = ts(T.dn[:, 0:48], T.ed[:, 0:48], 1.0, None, AL.min, None, [c_t])
+    c_2 = cp(T.cf[:, 2:4], T.ec[:, 0:65:64], [c_b, c_o])
+    c_m = ts(T.dm[:], T.ec[:, 0:64], 1.0, None, AL.min, None, [c_b])
+    c_u = cp(T.offs[:], T.jq[:, 0:32], [g_j, g_x])
+    keep["lm"] = ts(lm_, ci_, 8.0, 1.0 / 32, AL.is_lt, AL.max, [c_c])
+    a_jc = act(T.jc[:], j16, S, None, [g_j])
+    a_mu = act(mu_, T.ds[:, 15:16], -1.0, 129.0, [c_d], AF.Relu)
+    a_sq = square(T.ds, [c_d])
+    a_is = act(is_, ci_, S, None, [c_c])
+    a_c3 = act(c3_, ci_, AW, -3 * L4)
+    a_d4t = act(T.d4t[:], T.dn[:, 0:48], 5 * L1, -4 * L1, [c_n])
+    keep["ct"] = act(ct_, cs_, -4.0, ci_, [c_2])
+    a_k0 = act(k0_, mu_, -K * B16, K * (K + B16), [a_mu])
+    a_nb = act(nb_, mu_, B16, -B16, [a_mu])
+    a_d16 = steps(T.d16, T.ds, H, a_sq)
+    keep["c4"] = act(c4_, cs_, L4 - 4 * AW, c3_, [a_c3, c_2])
+    a_sg = act(sg_, ct_, 4.0, cs_, [keep["ct"]])
+    a_b0 = act(b0_, ct_, L1, -3 * L1, [keep["ct"]])
+    a_k1 = act(k1_, ci_, K, k0_, [a_k0])
+    keep["d4"] = [act(T.d4[:, 64 * j:64 * j + 64], T.dm[:], 5 * L4, -4 * L4, [c_m]) for j in range(H // 64)]
+    v_1 = ts(T.lt[:, 0:24], T.lab[:, 24:48], 32.0, None, AL.mult, None, [l_r])
+    v_2 = tt(T.lt[:, 24:48], T.lab[:, 0:24], T.jc[:], AL.add, [l_l, a_jc])
+    q_e = [q_eb(0)]
     q_u = quant(T.qu[:], T.su[:], T.us[:], [l_u])
-    v_1 = ts(T.lt[:, 0:72], T.lab[:, 72:144], 32.0, None, AL.mult, None, l_l[3:])
-    v_2 = tt(T.lt[:, 72:144], T.lab[:, 0:72], T.jc[:], AL.add, l_l[:3] + [a_jc])
-    p_u = cp(T.qr[:].bitcast(dt.uint32), T.qu[:].bitcast(dt.uint32).indirect(T.offu[:]), [q_u, k_u])
-    p_us = act(T.sr[:], T.su[:].indirect(T.offu[:]), 1.0, None, [q_u, k_u])
-    v_3 = tt(T.lt[:, 144:216], T.lt[:, 0:72], T.lt[:, 72:144], AL.add, [v_1, v_2])
-    a_x = act(T.xg[:], T.lt[:, 144:216].indirect(T.offx[:]), 1.0, None, [v_3, k_x])
-    a_nb = minus_sum(nb_, T.dt2[:, 0:16], T.dt1[:, 32:48], [k_b])
-    a_t4 = minus_sum(t4_, T.dt2[:, 16:20], T.dt1[:, 48:52], [k_b4])
-    a_jb = act(jb1_, nb_, -2.0, ci_, [a_nb])
-    a_c4 = act(c4_, ct_, AW, t4_, [a_t4])
-    a_jb1 = act(T.jb1[:], T.j16[:, 0:24], 1.0, jb1_, [a_jb])
-    q_x0 = quant(T.q1[:, 0:H], T.s1[:, 0:H], T.xs[:, 0:2 * C], [l_x0])
-    q_x1 = quant(T.q1[:, H:C], T.s1[:, H:C], T.xs[:, 2 * C:4 * C], [l_x1])
-    m_s = mm(0, T.qr[:], T.sr[:], T.q1[:], T.s1[:], C, [p_u, p_us, q_x0, q_x1])
+    v_3 = [tt(T.ta1[:, 64 * h:64 * h + 12], T.lt[:, h:24:2], T.lt[:, 24 + h:48:2], AL.add, [v_1, v_2, z_t[0]]) for h in range(2)]
+    q_e.append(q_eb(1))
+    p_u = cp(T.qr[:].bitcast(dt.uint32), T.qu[:].bitcast(dt.uint32).indirect(offu), [q_u, c_u])
+    p_us = act(T.sr[:], T.su[:].indirect(offu), 1.0, None, [q_u, c_u])
+    a_d16.append(act(T.d16[:, H:C], T.d16[:, 0:H], 1.0, None, a_d16))
+    a_jb1 = act(T.jb1[:], j16, K, k1_, [a_k1])
+    a_b1 = act(b1_, sg_, S, b0_, [a_sg, a_b0])
+    a_k2 = act(k2_, sg_, 2 * K, k0_, [a_sg])
+    q_x = quant(T.q1[:], T.s1[:], T.xs[:], [l_x])
+    m_s = mm(0, T.qr[:], T.sr[:], T.q1[:], T.s1[:], C, [p_u, p_us, q_x])
+    keep["jm"] = act(T.jm[:], j16, S, b1_, [a_b1])
+    a_jb2 = act(T.jb2[:, 0:24], T.j2[:], K, k2_, [a_k2, g_j2])
+    v_4 = spread_a("1", v_3)
     q_e += [q_eb(2), q_eb(3)]
+    v_5 = spread_b("1", v_4)
 
     def unpack(q, s, m, banks, deps):
         return [mm(banks[b], T.qe[:, 128 * b:128 * b + 128], T.se[:, 128 * b:128 * b + 128], q, s, m, deps[b] + [q_e[b]]) for b in range(4)]
 
     def evac(f, lo, m, banks, evs):
-        return [act(f[:, lo + b:lo + 4 * m:4], bank(banks[b], m), 0.5, None, [evs[b]]) for b in range(4)]
+        return [act(f[:, 4 * lo + b:4 * (lo + m):4], bank(banks[b], 0, m), 0.5, None, [evs[b]]) for b in range(4)]
 
-    def places(r, fl, jb, jdeps, extra, val):
-        fb, ys, yh, sm = T["fb" + r], T["ys" + r], T["yh" + r], T["sm" + r]
-        s = scan(ys[:, 0:C + 1], fb[:, C:2 * C + 1], fb[:, 0:C + 1], K, AL.add, AL.subtract, fl)
-        vdeps = extra(0)
-        tc = cp(sm[:, 72:73], ys[:, C:C + 1], [s])
-        if r == "1":
-            hs = [scan(yh[:], T.d16[:], ys[:, 0:C], 0.0, AL.add, AL.max, [s, a_d16])]
-        else:
-            hs = [scan(yh[:, H * k:H * k + H], T.d16[:, 0:H], ys[:, k:C:2], 0.0, AL.add, AL.max, [s, a_d16]) for k in range(2)]
-        jt = ts(sm[:, 0:24], jb, sm[:, 72:73], None, AL.add, None, [tc] + jdeps)
+    def flag(lo, step, in_, w, deps):
+        return ts(T.fb[:, w * (C + 1) + lo:w * (C + 1) + C:step], in_, 0.0, K + w, AL.is_gt, AL.mult, deps)
+
+    def count(deps):
+        return scan(T.ys[:], T.fb[:, C:2 * C], T.fb[:, 0:C], K, AL.add, AL.subtract, deps)
+
+    def hold(out, steps_, data, deps):
+        return scan(out, steps_, data, 0.0, AL.add, AL.max, deps)
+
+    def places(r, jt, hs, fills, val):
+        yh, sm = T["yh" + r], T["sm" + r]
         d = tt(sm[:, 24:48], sm[:, 0:24], yh[:, 15:C:16], AL.subtract, [jt] + hs)
-        mn = tt(sm[:, 48:72], sm[:, 24:48], yh[:, 15:C:16], AL.min, [d])
-        po = ts(T["pos" + r][:], sm[:, 48:72], nb_, None, AL.add, None, [mn, a_nb])
-        vdeps = vdeps + extra(1)
-        return cp(T["w" + r][:].indirect(T["pos" + r][:]), val, [po] + vdeps)
+        y0 = ts(sm[:, 48:72], yh[:, 15:C:16], nb_, None, AL.add, None, hs + [a_nb])
+        fills(0)
+        po = tt(T["pos" + r][:], sm[:, 24:48], sm[:, 48:72], AL.min, [d, y0])
+        return cp(T["w" + r][:].indirect(T["pos" + r][:]), val, [po] + fills(1))
 
-    def layer(r, sc, fdeps, mdeps, bdeps, between, early, gap, q, s):
+    mb = [5, 6, 7, 0]
+
+    def layer(r, sc, fdeps, mdeps, bdeps, hook, q, s, k):
         w, hw, im, fm = T["w" + r], T["hw" + r], T["im" + r], T["fm" + r]
         ol, oh, om = T["ol" + r], T["oh" + r], T["om" + r]
         f, fh, p, pp, z, t, vt = [T[x + r] for x in ("f", "fh", "p", "pp", "z", "t", "vt")]
-        sh = scan(hw[:, H:C], T.d4[:], w[:, 1:C:2], 0.0, AL.add, AL.max, [sc, a_d4])
-        early(0)
-        oh_ = ts(oh[:], hw[:, H + 3:C:4], c4_, 1.0 / AW, AL.add, AL.mult, [sh, a_c4])
-        gh = [act(fh[:, C * k:C * k + C], f[:].indirect(oh[:, 24 * k:24 * k + 24]), 1.0, None, [oh_] + fdeps) for k in range(2)]
-        between()
+        qz, sz = T["qz" + r], T["sz" + r]
+        a4, h4 = 4 * NA, 4 * H
+        hook("ordered", None)
+        sh = scan(hw[:, H:C], T.d4[:], w[:, 1:C:2], 0.0, AL.add, AL.max, [sc] + keep["d4"])
         sl = scan(hw[:, 0:H], T.d4[:], w[:, 0:C:2], 0.0, AL.add, AL.max, [sc])
-        early(1)
-        i0 = cp(im[:, 0:96], hw[:, 3:C:4], [sh, sl])
+        hook("held", None)
+        oh_ = ts(oh[:], hw[:, H + 3:C:4], c4_, 1.0 / AW, AL.add, AL.mult, [sh, keep["c4"]])
+        gh = [act(fh[:, 256 * j:256 * j + 256], f[:].indirect(oh[:, 16 * j:16 * j + 16]), 1.0, None, [oh_] + fdeps) for j in range(3)]
+        hook("right", None)
+        i2 = ts(im[:, 1:96:2], hw[:, H + 3:C:4], 31, None, AL.bitwise_and, None, [sh])
+        i1 = ts(im[:, 0:96:2], hw[:, 3:H:4], 3, 124, AL.logical_shift_right, AL.bitwise_and, [sl])
         ol_ = ts(ol[:], hw[:, 3:H:4], c4_, 1.0 / AW, AL.add, AL.mult, [sl])
-        i1 = ts(im[:, 96:144], im[:, 0:48], 31 * 32, None, AL.bitwise_and, None, [i0])
-        i2 = ts(im[:, 144:192], im[:, 48:96], 31, None, AL.bitwise_and, None, [i0])
-        i3 = ts(fm[:, 0:48], im[:, 96:144], I / 32.0, None, AL.mult, None, [i1])
-        mx = [tt(p[:, 0:C], f[:].indirect(ol[:, 0:24]), fh[:, 0:C], AL.max, [ol_, gh[0]] + fdeps)]
-        i4 = tt(fm[:, 48:96], fm[:, 0:48], im[:, 144:192], AL.add, [i3, i2])
-        mx.append(tt(p[:, C:2 * C], f[:].indirect(ol[:, 24:48]), fh[:, C:2 * C], AL.max, [ol_, gh[1]]))
-        om_ = ts(om[:], fm[:, 48:96], 4.0, ct_, AL.mult, AL.add, [i4])
-        a_p = act(pp[:], p[:], 64.0, None, mx)
-        zz = tt(z[:], T.mf[:].indirect(om[:]), p[:], AL.add, mx + [om_] + mdeps())
-        qz = quant(T["qz" + r][:], T["sz" + r][:], z[:], [zz])
-        rr = [mm(1 + b, T.qw[:, 128 * b:128 * b + 128], T.sw[:, 128 * b:128 * b + 128], T["qz" + r][:], T["sz" + r][:], H,
-                 [qz, l_w, l_ws] + bdeps) for b in range(4)]
-        gap()
-        ad = [tt(t[:, b:4 * H:4], bank(1 + b, H), pp[:, b:4 * H:4], AL.add, [rr[b], a_p]) for b in range(4)]
-        sv = [act(vt[:, b:4 * H:4], t[:, b:4 * H:4], 0.03125, None, [ad[b]]) for b in range(3)]
-        sv.append(ts(vt[:, 3:4 * H:4], t[:, 3:4 * H:4], 0.03125, None, AL.mult, None, [ad[3]]))
-        return quant(q, s, vt[:], sv), ad
+        hook("lists", [sh, sl])
+        i3 = scan(fm[:], T.five[:], im[:], 0.0, AL.mult, AL.add, [i1, i2, g_5])
+        hook("sum", None)
 
-    keep = {}
-    mb = [5, 6, 7, 0]
-    a_d4 = act(T.d4[:], T.ds[:, 16:32].indirect(T.offt[:]), 1.0, None, [k_d, k_ot])
-    m_d = unpack(T.q1[:], T.s1[:], C, [1, 2, 3, 4], [[]] * 4)
-    fl = flags("1", 0, 0, 1, C, [m_s])
-    e_f = evac(T.f1, 0, C, [1, 2, 3, 4], m_d)
+        def most(j):
+            return tt(p[:, 256 * j:256 * j + 256], f[:].indirect(ol[:, 16 * j:16 * j + 16]), fh[:, 256 * j:256 * j + 256], AL.max, [ol_, gh[j]] + fdeps)
+
+        def weights(banks, lo, deps):
+            return [mm(banks[b], T.qw[:, 128 * b:128 * b + 128], T.sw[:, 128 * b:128 * b + 128], qz[:, lo:lo + 128], sz[:, lo:lo + 128], 128,
+                       deps + [l_w, l_ws]) for b in range(4)]
+
+        def plus(banks, at, lo, hi, rr, dep):
+            return [tt(t[:, lo + b:hi:4], bank(banks[b], at, 128), pp[:, lo + b:hi:4], AL.add, [rr[b], dep]) for b in range(4)]
+
+        mx = [most(0)]
+        om_ = ts(om[:], fm[:, 1:96:2], 4.0, ct_, AL.mult, AL.add, [i3, keep["ct"]])
+        hook("most 0", None)
+        mx.append(most(1))
+        hook("most 1", None)
+        pa = act(pp[:, 0:a4], p[:, 0:a4], 64.0, None, mx)
+        mx.append(most(2))
+        pb = act(pp[:, a4:h4], p[:, a4:h4], 64.0, None, [mx[2]])
+        za = tt(z[:, 0:a4], T.mf[:].indirect(om[:, 0:NA // 4]), p[:, 0:a4], AL.add, mx[0:2] + [om_] + mdeps)
+        zb = tt(z[:, a4:h4], T.mf[:].indirect(om[:, NA // 4:H // 4]), p[:, a4:h4], AL.add, [mx[2]])
+        ra = weights([1, 2, 3, 4], 0, [quant(qz[:, 0:128], sz[:, 0:128], z[:, 0:512], [za])])
+        hook("gap a", None)
+        rb = weights(mb, 128, [quant(qz[:, 128:256], sz[:, 128:256], z[:, h4 - 512:h4], [zb])] + bdeps)
+        hook("gap b", None)
+        ad = plus([1, 2, 3, 4], 0, 0, a4, ra, pa)
+        sv = [act(vt[:, b:a4:4], t[:, b:a4:4], 0.03125, None, [ad[b]]) for b in range(4)]
+        bd = plus(mb, 128 - (H - NA), a4, h4, rb, pb)
+        hook("added", None)
+        sv.append(ts(vt[:, a4:h4], t[:, a4:h4], 0.03125, None, AL.mult, None, bd))
+        hook("scaled", None)
+        va = quant(q[:, H:C], s[:, H:C], vt[:], sv)
+        push(k, q[:, 0:H].bitcast(dt.uint8), q[:, H:C].bitcast(dt.uint8), "rq" + r, [va])
+        push(k, s[:, 0:H], s[:, H:C], "rq" + r, [va])
+        return va
+
     e_m = []
 
-    def extra1(k):
+    def mid(k, deps):
+        lo, m = cut[k], cut[k + 1] - cut[k]
+        q_m = quant(T.qm[:, lo:lo + m], T.sm[:, lo:lo + m], T.ms[:, 4 * lo:4 * (lo + m)], [l_m[k]])
+        e_m.extend(evac(T.mf, lo, m, mb, unpack(T.qm[:, lo:lo + m], T.sm[:, lo:lo + m], m, mb, [d + [q_m] for d in deps])))
+
+    v_6 = spread_c("1", v_5)
+    a_x = act(T.xg1[:], T.tc1[:].indirect(offx), 1.0, is_, [v_6, c_u, a_is])
+    e_f = evac(T.f1, 0, C, [1, 2, 3, 4], unpack(T.q1[:], T.s1[:], C, [1, 2, 3, 4], [[]] * 4))
+    f1 = [flag(0, 1, bank(0, 0, C), w, [m_s]) for w in range(2)]
+    n1 = total(T.sm1[:, 72:73], T.fb[:, 0:C], [f1[0]])
+    s1 = count(f1 + [z_f])
+    mid(0, [f1] * 4)
+    h1 = hold(T.yh1[:], T.d16[:], T.ys[:], [s1] + a_d16)
+    jt = ts(T.sm1[:, 0:24], T.jb1[:], T.sm1[:, 72:73], 1.0 / K, AL.add, AL.mult, [n1, a_jb1])
+    mid(1, [[e] for e in e_m])
+
+    def fills1(k):
         if k == 0:
-            return [op("V", lambda q: q.transpose(T.val1[:], T.xg[:]), [a_x])]
-        q_m = quant(T.qm[:], T.sm[:], T.ms[:], [l_m])
-        keep["mm"] = unpack(T.qm[:], T.sm[:], NM, mb, [[q_m], [], [], [fl[0]]])
-        for b in range(2):
-            e_m.append(act(T.mf[:, b:4 * NM:4], bank(mb[b], NM), 0.5, None, [keep["mm"][b]]))
-        return []
+            keep["vt"] = turn(T.val1[:], T.xg1[:], [a_x])
+        return [keep["vt"]]
 
-    sc = places("1", fl + [z_f[0]], T.jb1[:], [a_jb1], extra1, T.val1[:])
+    sc = places("1", jt, [h1], fills1, T.val1[:])
 
-    def between1():
-        for b in (2, 3):
-            e_m.append(act(T.mf[:, b:4 * NM:4], bank(mb[b], NM), 0.5, None, [keep["mm"][b]]))
+    def hook1(at, held):
+        if at == "lists":
+            keep["xa"] = ts(T.xa[:, 0:48], T.hw1[:, 3:H:4], 31, None, AL.bitwise_and, None, held)
+            keep["xb"] = ts(T.xa[:, 48:96], T.hw1[:, H + 3:C:4], 31 * 32, None, AL.bitwise_and, None, held)
+        if at == "sum":
+            keep["xs"] = tt(T.xb[:, 0:48], T.xa[:, 0:48], T.xa[:, 48:96], AL.add, [keep["xa"], keep["xb"]])
+        if at == "most 0":
+            keep["xh"] = scan(T.xb[:, 48:96], T.d4t[:], T.xb[:, 0:48], 0.0, AL.add, AL.max, [keep["xs"], a_d4t])
+        if at == "most 1":
+            push(0, T.xd[:], T.xc[:], "rl1", [tt(T.xc[:], T.xb[:, 51:96:4], T.jm[:, 0:12], AL.add, [keep["xh"], keep["jm"]])])
+        if at == "gap a":
+            keep["s0"] = ts(T.ee[:, 0:64], T.ic[:], sg_, None, AL.add, None, [g_c, a_sg])
+        if at == "gap b":
+            keep["o"] = [tt(T.ta2[:, 64 * h + 6:64 * h + 12], T.xb[:, 51 + 4 * h:96:8], T.jm[:, 12 + h:24:2], AL.add, [keep["xh"], z_t[1]])
+                         for h in range(2)]
+            keep["s1"] = ts(T.ee[:, 64:128], T.ee[:, 0:64], 15, None, AL.bitwise_and, None, [keep["s0"]])
+        if at == "added":
+            keep["cp"] = ts(T.dp[:, 0:64], T.ee[:, 64:128], 0.0695, 128.465, AL.mult, AL.add, [keep["s1"]])
 
-    def early1(k):
-        if k == 0:
-            keep["iw"] = cp(T.iw[:], T.w1[:], [sc])
-            return
-        keep["xa"] = ts(T.xa[:], T.iw[:, 0:C:2], 31, None, AL.bitwise_and, None, [keep["iw"]])
-        keep["xb"] = ts(T.xb[:], T.iw[:, 1:C:2], 31 * 32, None, AL.bitwise_and)
-        for d in (keep["xa"], keep["xb"], g_b):
-            wait("G", d)
-        rid, pid, _e = topo.addr(dst[0])
-        g.remote_dma_fused([RemoteDMATransfer(dst_ids=[DstId(rid=rid, pnc=pid)], dma_engine_mask=lanes(core), remote_sem=T.sem["rl1"],
-                                              srcs=[T.xa[:], T.xb[:], T.base[:, 0:H]], dsts=[T.val2[:, 0:H]], alu_op=1)],
-                           local_sem=T.sem["sent"])
-        sent[0] += width(core)
+    va1 = layer("1", sc, e_f, e_m, e_m, hook1, T.q2, T.s2, 0)
 
-    def gap1():
-        keep["o1"] = tt(T.xc[:], T.xa[:], T.xb[:], AL.add, [keep["xa"], keep["xb"]])
-
-    q_v1, ad1 = layer("1", sc, e_f, lambda: e_m, e_f, between1, early1, gap1, T.q2[:, H:C], T.s2[:, H:C])
-    push(0, T.q2[:, 0:H].bitcast(dt.uint8), T.q2[:, H:C].bitcast(dt.uint8), "rq1", [q_v1])
-    push(0, T.s2[:, 0:H], T.s2[:, H:C], "rq1", [q_v1])
-
-    m_so = mm(5, T.qr[:], T.sr[:], T.q2[:, H:C], T.s2[:, H:C], H, [q_v1, e_m[0]])
+    m_so = mm(5, T.qr[:], T.sr[:], T.q2[:, H:C], T.s2[:, H:C], H, [va1])
     m_do = unpack(T.q2[:, H:C], T.s2[:, H:C], H, [1, 2, 3, 4], [[]] * 4)
-    z_f[1] = fill(T.fb2[:, C:C + 1], 0.0)
-    k_jb = ts(jb2_, ci_, nb_, 2.0, AL.subtract, AL.mult, [a_nb])
-    o_2 = tt(T.val2[:, H:C], T.xc[:], T.base[:, H:C], AL.add, [keep["o1"], g_b])
-    flo = flags("2", 5, 1, 2, H, [m_so])
-    k_jb2 = ts(T.jb2[:], T.j2[:], jb2_, None, AL.add, None, [k_jb, g_j2])
-    e_o = evac(T.f2, 4 * H, H, [1, 2, 3, 4], m_do)
+    a_ds = steps(T.d16s, T.dp, H, square(T.dp, [keep["cp"]]))
+    o_a = [cp(T.ta2[:, 64 * h:64 * h + 6], T.xd[:, h:12:2], [("rl1", width(src[0])), z_t[1]]) for h in range(2)]
+    o_4 = spread_a("2", o_a + keep["o"])
+    fo = [flag(1, 2, bank(5, 0, H), w, [m_so]) for w in range(2)]
+    o_5 = spread_b("2", o_4)
+    n2 = total(T.sm2[:, 73:74], T.fb[:, 1:C:2], [fo[0]])
+    o_6 = spread_c("2", o_5)
+    a_y = act(T.xg2[:], T.tc2[:].indirect(offx), 1.0, None, [o_6])
+    e_o = evac(T.f2, H, H, [1, 2, 3, 4], m_do)
+    j_o = ts(T.jb2[:, 24:48], T.jb2[:, 0:24], T.sm2[:, 73:74], None, AL.add, None, [n2, a_jb2])
+    v_u = turn(T.val2[:], T.xg2[:], [a_y])
 
     r1 = ("rq1", 2 * width(src[0]))
-    m_sa = mm(6, T.qr[:], T.sr[:], T.q2[:, 0:H], T.s2[:, 0:H], H, [r1, e_m[1]])
-    m_da = unpack(T.q2[:, 0:H], T.s2[:, 0:H], H, [1, 2, 3, 4], [[e] for e in e_o])
-    fla = flags("2", 6, 0, 2, H, [m_sa])
-    e_a = evac(T.f2, 0, H, [1, 2, 3, 4], m_da)
-    sc2 = places("2", fla + flo + [z_f[1]], T.jb2[:], [k_jb2], lambda k: [[], [o_2, ("rl1", width(src[0]))]][k], T.val2[:])
+    m_sa = mm(6, T.qr[:], T.sr[:], T.q2[:, 0:H], T.s2[:, 0:H], H, [r1])
+    l_v = dma("S", T.vs[:], T.v[:], [m_sa])
+    e_a = evac(T.f2, 0, H, [1, 2, 3, 4], unpack(T.q2[:, 0:H], T.s2[:, 0:H], H, [1, 2, 3, 4], [[e] for e in e_o]))
+    fa = [flag(0, 2, bank(6, 0, H), w, [m_sa]) for w in range(2)]
+    n3 = total(T.sm2[:, 72:73], T.fb[:, 0:C:2], [fa[0]])
+    s2 = count(fa + fo)
+    jt2 = ts(T.sm2[:, 0:24], T.jb2[:, 24:48], T.sm2[:, 72:73], 1.0 / K, AL.add, AL.mult, [n3, j_o])
+    h2 = [hold(T.yh2[:, H * k:H * k + H], T.d16s[:], T.ys[:, k:C:2], [s2] + a_ds) for k in range(2)]
+    sc2 = places("2", jt2, h2, lambda k: [v_u], T.val2[:])
 
-    def between2():
-        a1 = act(T.wd[:, H:C], T.w2[:, 1:C:2], 1.0, None, [sc2])
-        keep["lw"] = dma("S", T.lw[:], T.wd[0:128:16, :], [keep["a0"], a1])
-        push(1, T.lwr[:], T.lw[:], "rl2", [keep["lw"]])
-
-    def early2(k):
-        if k == 0:
+    def hook2(at, held):
+        if at == "ordered":
             keep["a0"] = act(T.wd[:, 0:H], T.w2[:, 0:C:2], 1.0, None, [sc2])
+            keep["a1"] = act(T.wd[:, H:C], T.w2[:, 1:C:2], 1.0, None, [sc2])
+        if at == "right":
+            keep["lw"] = dma("S", T.lw[:], T.wd[0:128:16, :], [keep["a0"], keep["a1"]])
+            push(1, T.lwr[:], T.lw[:], "rl2", [keep["lw"]])
+            a_h = act(ih_, ci_, 0.5)
+            keep["fq"] = act(fq_, co_, H - 0.5, ih_, [a_h])
+        if at == "gap a":
+            keep["of"] = ts(T.offf[:], j16, 0.5, fq_, AL.mult, AL.add, [keep["fq"]])
+        if at == "gap b":
+            keep["qv"] = quant(T.qv[:], T.sv[:], T.vs[:], [l_v])
+        if at == "added":
+            keep["u0"] = ts(T.lri[:, 1:48:2], T.lw[:], lm_, -0.3, AL.mult, AL.add, [keep["lm"], keep["lw"]])
 
-    def gap2():
-        keep["qv"] = quant(T.qv[:], T.sv[:], T.vs[:], [l_v])
+    va2 = layer("2", sc2, e_o + e_a, [], [], hook2, T.q3, T.s3, 1)
 
-    q_v2, ad2 = layer("2", sc2, e_o + e_a, lambda: [], e_a, between2, early2, gap2, T.q3[:, H:C], T.s3[:, H:C])
-    push(1, T.q3[:, 0:H].bitcast(dt.uint8), T.q3[:, H:C].bitcast(dt.uint8), "rq2", [q_v2])
-    push(1, T.s3[:, 0:H], T.s3[:, H:C], "rq2", [q_v2])
-
-    m_yo = mm(5, T.qv[:], T.sv[:], T.q3[:, H:C], T.s3[:, H:C], H, [q_v2, keep["qv"], flo[0]])
-    c4 = ts(T.ci[:, 4:5], T.pcol[:], 3, 1, AL.logical_shift_right, AL.bitwise_and)
-    c5 = ts(T.ci[:, 5:6], T.pcol[:], 1, None, AL.bitwise_and)
-    c6 = ts(T.ci[:, 6:7], T.pcol[:], 1, 7, AL.logical_shift_right, AL.bitwise_and)
-    k_c2 = cp(T.cf[:, 4:7], T.ci[:, 4:7], [c4, c5, c6])
-    k_lm = ts(lm_, T.cf[:, 4:5], -31.0 / 32.0, 1.0, AL.mult, AL.add, [k_c2])
-    k_la = ts(la_, T.cf[:, 4:5], -0.3, None, AL.mult)
-    k_fq = ts(fq_, T.cf[:, 5:6], float(H), T.cf[:, 6:7], AL.mult, AL.add)
-    k_of = ts(T.offf[:], T.j16[:, 0:24], 0.5, fq_, AL.mult, AL.add, [k_fq])
-    u_0 = ts(T.lri[:, 1:48:2], T.lw[:], lm_, la_, AL.mult, AL.add, [k_lm, k_la, keep["lw"]])
-    u_1 = ts(T.lri[:, 0:48:2], T.lwr[:], lm_, la_, AL.mult, AL.add, [("rl2", width(src[1]))])
-    u_2 = ts(T.lrj[:], T.lri[:], 31, None, AL.bitwise_and, None, [u_0, u_1])
+    done = []
+    m_yo = mm(5, T.qv[:], T.sv[:], T.q3[:, H:C], T.s3[:, H:C], H, [va2, keep["qv"]])
+    u_1 = ts(T.lri[:, 0:48:2], T.lwr[:], lm_, -0.3, AL.mult, AL.add, [("rl2", width(src[1]))])
+    u_2 = ts(T.lrj[:], T.lri[:], 31, None, AL.bitwise_and, None, [keep["u0"], u_1])
     u_3 = cp(T.lrf[:], T.lrj[:], [u_2])
-    dma("S", T.lr[:], T.lrf[:], [u_3])
-    y_o = act(T.yb[:, 1:C:2], bank(5, H), 1.0, None, [m_yo])
-
+    done.append(dma("S", T.lr[:], T.lrf[:], [u_3]))
+    y_o = act(T.yb[:, 1:C:2], bank(5, 0, H), 1.0, None, [m_yo])
     r2 = ("rq2", 2 * width(src[1]))
-    m_ya = mm(6, T.qv[:], T.sv[:], T.q3[:, 0:H], T.s3[:, 0:H], H, [r2, fla[0]])
-    p_s = act(T.so[:], T.s3[:].indirect(T.offf[:]), 1.0, None, [r2, q_v2, k_of])
-    p_c = cp(T.qo[:].bitcast(dt.uint32), T.q3[:].bitcast(dt.uint32).indirect(T.offf[:]), [r2, q_v2, k_of])
-    dma("S", T.oc[:], T.qo[:].bitcast(dt.uint8), [p_c])
-    dma("S", T.y[:], T.yb[:], [cp(T.yb[:, 0:C:2], bank(6, H), [m_ya]), y_o])
+    m_ya = mm(6, T.qv[:], T.sv[:], T.q3[:, 0:H], T.s3[:, 0:H], H, [r2, keep["qv"]])
+    p_s = act(T.so[:], T.s3[:].indirect(T.offf[:]), 1.0, None, [r2, va2, keep["of"]])
+    p_c = cp(T.qo[:].bitcast(dt.uint32), T.q3[:].bitcast(dt.uint32).indirect(T.offf[:]), [r2, va2, keep["of"]])
+    done.append(dma("S", T.oc[:], T.qo[:].bitcast(dt.uint8), [p_c]))
+    done.append(dma("S", T.y[:], T.yb[:], [cp(T.yb[:, 0:C:2], bank(6, 0, H), [m_ya]), y_o]))
     for k in range(4):
-        dma("A" if k < 3 else "S", T.osc[4 * k:4 * k + 4, :], T.so[32 * k:32 * k + 4, :], [p_s])
+        done.append(dma("A" if k < 3 else "S", T.osc[4 * k:4 * k + 4, :], T.so[32 * k:32 * k + 4, :], [p_s]))
+    op("G", None, [("sent", sent[0])] + done, 0)
 
-    wait("G", ("sent", sent[0]))
-    for name in order:
-        if max(waited[e].get(name, 0) for e in queues) < count[name]:
-            wait("G", (name, count[name]))
+    known = {e: set() for e in queues}
+    behind, waits, needed = [], [], set()
+    for e, call, deps, inc in calls:
+        mine = []
+        for d in sorted(set(deps), key=lambda x: -x if isinstance(x, int) else 1):
+            if d not in known[e]:
+                mine.append(d)
+                needed.add(d)
+                known[e].add(d)
+                if isinstance(d, int):
+                    known[e].update(behind[d])
+        waits.append(mine)
+        behind.append(set(known[e]))
+    pool = {e: [] for e in queues}
+    event, used = {}, [0]
+    for j, (e, call, deps, inc) in enumerate(calls):
+        for d in waits[j]:
+            name, c = event[d] if isinstance(d, int) else d
+            queues[e].wait_ge(T.sem[name], c)
+        if call is None:
+            continue
+        ins = call(queues[e])
+        if j in needed:
+            free = [x for x in pool[e] if x[2] in behind[j]] if inc == 1 else []
+            if free:
+                slot = free[0]
+            else:
+                slot = ["e%d" % used[0], 0, j]
+                used[0] += 1
+                if inc == 1:
+                    pool[e].append(slot)
+            slot[1] += inc
+            slot[2] = j
+            ins.then_inc(T.sem[slot[0]], inc)
+            event[j] = (slot[0], slot[1])

@@ -4,6 +4,9 @@ from concourse.mybir import dt, AluOpType, ActivationFunctionType, AxisListType
 C = 384
 H = C // 2
 NA = 128
+NB = H - NA
+QW = 2 * NA + 128 + NB
+OB = QW - 2 * NB
 NM = 400
 HALF = "float16"
 X4 = "float8_e4m3fn_x4"
@@ -22,7 +25,8 @@ def _sb(n, d):
 SCRATCH = {
     "ps": ("psum", [128, 4096], "float32"),
     "xs": _sb(4 * C, "bfloat16"), "us": _sb(512, "bfloat16"), "vs": _sb(512, "bfloat16"), "ms": _sb(4 * NM, "bfloat16"),
-    "q1": _sb(C, X4), "s1": _sb(C, "uint8"), "q2": _sb(C, X4), "s2": _sb(C, "uint8"), "q3": _sb(C, X4), "s3": _sb(C, "uint8"),
+    "q1": _sb(C, X4), "s1": _sb(C, "uint8"), "q2": _sb(C, X4), "s2": _sb(C, "uint8"), "q3": _sb(QW, X4), "s3": _sb(QW, "uint8"),
+    "qs": _sb(256, X4), "ss": _sb(256, "uint8"),
     "qo": _sb(C, X4), "so": _sb(C, "uint8"),
     "qu": _sb(128, X4), "su": _sb(128, "uint8"), "qr": _sb(128, X4), "sr": _sb(128, "uint8"),
     "qv": _sb(128, X4), "sv": _sb(128, "uint8"), "qm": _sb(NM, X4), "sm": _sb(NM, "uint8"),
@@ -33,7 +37,7 @@ SCRATCH = {
     "ds": _sb(128, "bfloat16"), "dm": _sb(64, "bfloat16"), "dn": _sb(64, "bfloat16"), "dp": _sb(128, "bfloat16"),
     "cf": _sb(4, "float32"), "cd": _sb(24, "float32"),
     "jq": _sb(48, "float32"), "j2": _sb(24, "float32"), "five": _sb(96, "float32"), "jm": _sb(24, "float32"),
-    "d16": _sb(C, "bfloat16"), "d4": _sb(H, "bfloat16"), "d4t": _sb(48, "bfloat16"), "d16s": _sb(H, "bfloat16"),
+    "d16": _sb(C, "bfloat16"), "d4": _sb(H, "bfloat16"), "d4t": _sb(48, "bfloat16"), "d16s": _sb(C, "bfloat16"),
     "offs": _sb(32, "uint16"), "offf": _sb(24, "uint16"),
     "lab": _sb(48, "int32"), "lt": _sb(48, "float32"), "jc": _sb(24, "float32"), "jb1": _sb(24, "float32"), "jb2": _sb(48, "float32"),
     "mf": _sb(4 * NM, "bfloat16"),
@@ -41,7 +45,7 @@ SCRATCH = {
     "xa": _sb(96, "int32"), "xb": _sb(96, "float32"), "xc": _sb(12, "float32"), "xd": _sb(12, "float32"),
     "wd": _sb(C, "float32"), "lw": _sb(24, "float32"), "lwr": _sb(24, "float32"),
     "lri": _sb(48, "int32"), "lrj": _sb(48, "int32"), "lrf": _sb(48, "float32"),
-    "yb": _sb(C, "float32"),
+    "yb": _sb(C, "float32"), "ca": _sb(48, HALF), "cb": _sb(48, HALF), "cc": _sb(72, "float32"),
 }
 for _r in ("1", "2"):
     SCRATCH.update({
@@ -56,7 +60,7 @@ for _r in ("1", "2"):
         "qz" + _r: _sb(256, X4), "sz" + _r: _sb(256, "uint8"),
     })
 NSEM = 140
-SEMAPHORES = ["e%d" % k for k in range(NSEM)] + ["rq1", "rq2", "rl1", "rl2", "sent"]
+SEMAPHORES = ["e%d" % k for k in range(NSEM)] + ["rq1", "ra2", "rb2", "rl1", "rl2", "rc1", "sent"]
 
 AL = AluOpType
 AF = ActivationFunctionType
@@ -149,16 +153,16 @@ def rank_program(g, core, T, topo):
 
     z_e = fill(T.eb[:], 0.0)
     g_a = iota(T.ia[:], [[-1, 64]], 64, 1, False)
-    g_b = iota(T.ib[:], [[-4, 64]], 256, 1, False)
     g_j = iota(T.jq[:, 24:48], [[16, 24]], 0, 0, True)
-    g_x = iota(T.jq[:, 0:24], [[1, 12], [-32, 2]], 32, 0, True)
     g_e = op("G", lambda q: q.affine_select(T.eb[:, 3:515:4], T.eb[:, 3:515:4], [[1, 128]], AL.not_equal, 1.0, 0, -1), [z_e])
+    g_x = iota(T.jq[:, 0:24], [[1, 12], [-32, 2]], 32, 0, True)
+    g_b = iota(T.ib[:], [[-4, 64]], 256, 1, False)
     g_j2 = iota(T.j2[:], [[1, 2], [32, 12]], 0, 0, True)
     g_5 = iota(T.five[:], [[0, 48], [5, 2]], 0, 0, True)
     g_c = iota(T.ic[:], [[-1, 64]], 64, 0, False)
     j16, offx, offu = T.jq[:, 24:48], T.offs[:, 0:24], T.offs[:, 24:32]
     ci_, cs_, co_ = T.cf[:, 0:1], T.cf[:, 2:3], T.cf[:, 3:4]
-    mu_, nb_, is_, k0_, k1_, k2_, ct_, c3_, c4_, lm_, ih_, fq_, sg_, b0_, b1_ = [T.cd[:, k:k + 1] for k in range(15)]
+    mu_, nb_, is_, k0_, k1_, k2_, ct_, c3_, c4_, lm_, ih_, fq_, sg_, b0_, b1_, ig_, fr_ = [T.cd[:, k:k + 1] for k in range(17)]
     keep = {}
 
     def q_eb(b):
@@ -186,46 +190,49 @@ def rank_program(g, core, T, topo):
     c_o = ts(T.ec[:, 64:65], T.ia[:, 0:1], 1, None, AL.bitwise_and)
     c_t = ts(T.ed[:, 0:48], T.ia[:, 0:48], 3, None, AL.bitwise_and)
     c_d = ts(T.ds[:, 0:64], T.ea[:], 0.0695, 128.465, AL.mult, AL.add, [c_a])
-    c_b = ts(T.ec[:, 0:64], T.ib[:], 2, 3, AL.logical_shift_right, AL.bitwise_and, [g_b])
     c_c = cp(ci_, T.ea[:, 0:1], [c_a])
     c_n = ts(T.dn[:, 0:48], T.ed[:, 0:48], 1.0, None, AL.min, None, [c_t])
-    c_2 = cp(T.cf[:, 2:4], T.ec[:, 0:65:64], [c_b, c_o])
-    c_m = ts(T.dm[:], T.ec[:, 0:64], 1.0, None, AL.min, None, [c_b])
-    c_u = cp(T.offs[:], T.jq[:, 0:32], [g_j, g_x])
-    keep["lm"] = ts(lm_, ci_, 8.0, 1.0 / 32, AL.is_lt, AL.max, [c_c])
     a_jc = act(T.jc[:], j16, S, None, [g_j])
     a_mu = act(mu_, T.ds[:, 15:16], -1.0, 129.0, [c_d], AF.Relu)
     a_sq = square(T.ds, [c_d])
     a_is = act(is_, ci_, S, None, [c_c])
     a_c3 = act(c3_, ci_, AW, -3 * L4)
     a_d4t = act(T.d4t[:], T.dn[:, 0:48], 5 * L1, -4 * L1, [c_n])
-    keep["ct"] = act(ct_, cs_, -4.0, ci_, [c_2])
     a_k0 = act(k0_, mu_, -K * B16, K * (K + B16), [a_mu])
     a_nb = act(nb_, mu_, B16, -B16, [a_mu])
     a_d16 = steps(T.d16, T.ds, H, a_sq)
-    keep["c4"] = act(c4_, cs_, L4 - 4 * AW, c3_, [a_c3, c_2])
-    a_sg = act(sg_, ct_, 4.0, cs_, [keep["ct"]])
-    a_b0 = act(b0_, ct_, L1, -3 * L1, [keep["ct"]])
     a_k1 = act(k1_, ci_, K, k0_, [a_k0])
-    keep["d4"] = [act(T.d4[:, 64 * j:64 * j + 64], T.dm[:], 5 * L4, -4 * L4, [c_m]) for j in range(H // 64)]
-    v_1 = ts(T.lt[:, 0:24], T.lab[:, 24:48], 32.0, None, AL.mult, None, [l_r])
-    v_2 = tt(T.lt[:, 24:48], T.lab[:, 0:24], T.jc[:], AL.add, [l_l, a_jc])
-    q_e = [q_eb(0)]
-    q_u = quant(T.qu[:], T.su[:], T.us[:], [l_u])
-    v_3 = [tt(T.ta1[:, 64 * h:64 * h + 12], T.lt[:, h:24:2], T.lt[:, 24 + h:48:2], AL.add, [v_1, v_2, z_t[0]]) for h in range(2)]
-    q_e.append(q_eb(1))
-    p_u = cp(T.qr[:].bitcast(dt.uint32), T.qu[:].bitcast(dt.uint32).indirect(offu), [q_u, c_u])
-    p_us = act(T.sr[:], T.su[:].indirect(offu), 1.0, None, [q_u, c_u])
     a_d16.append(act(T.d16[:, H:C], T.d16[:, 0:H], 1.0, None, a_d16))
     a_jb1 = act(T.jb1[:], j16, K, k1_, [a_k1])
+    keep["lm"] = ts(lm_, ci_, 8.0, 1.0 / 32, AL.is_lt, AL.max, [c_c])
+    q_e = [q_eb(0)]
+    v_1 = ts(T.lt[:, 0:24], T.lab[:, 24:48], 32.0, None, AL.mult, None, [l_r])
+    c_u = cp(T.offs[:], T.jq[:, 0:32], [g_j, g_x])
+    q_e.append(q_eb(1))
+    v_2 = tt(T.lt[:, 24:48], T.lab[:, 0:24], T.jc[:], AL.add, [l_l, a_jc])
+    q_e.append(q_eb(2))
+    c_b = ts(T.ec[:, 0:64], T.ib[:], 2, 3, AL.logical_shift_right, AL.bitwise_and, [g_b])
+    q_u = quant(T.qu[:], T.su[:], T.us[:], [l_u])
+    v_3 = [tt(T.ta1[:, 64 * h:64 * h + 12], T.lt[:, h:24:2], T.lt[:, 24 + h:48:2], AL.add, [v_1, v_2, z_t[0]]) for h in range(2)]
+    c_2 = cp(T.cf[:, 2:4], T.ec[:, 0:65:64], [c_b, c_o])
+    c_m = ts(T.dm[:], T.ec[:, 0:64], 1.0, None, AL.min, None, [c_b])
+    p_u = cp(T.qr[:].bitcast(dt.uint32), T.qu[:].bitcast(dt.uint32).indirect(offu), [q_u, c_u])
+    p_us = act(T.sr[:], T.su[:].indirect(offu), 1.0, None, [q_u, c_u])
+    keep["ct"] = act(ct_, cs_, -4.0, ci_, [c_2])
+    keep["c4"] = act(c4_, cs_, L4 - 4 * AW, c3_, [a_c3, c_2])
+    keep["d4"] = [act(T.d4[:, 64 * j:64 * j + 64], T.dm[:], 5 * L4, -4 * L4, [c_m]) for j in range(H // 64)]
+    a_sg = act(sg_, ct_, 4.0, cs_, [keep["ct"]])
+    a_b0 = act(b0_, ct_, L1, -3 * L1, [keep["ct"]])
+    m_s = []
+    for h in range(2):
+        q_x = quant(T.q1[:, H * h:H * h + H], T.s1[:, H * h:H * h + H], T.xs[:, 4 * H * h:4 * H * h + 4 * H], [l_x])
+        m_s.append(mm(5 * h, T.qr[:], T.sr[:], T.q1[:, H * h:H * h + H], T.s1[:, H * h:H * h + H], H, [p_u, p_us, q_x]))
     a_b1 = act(b1_, sg_, S, b0_, [a_sg, a_b0])
-    a_k2 = act(k2_, sg_, 2 * K, k0_, [a_sg])
-    q_x = quant(T.q1[:], T.s1[:], T.xs[:], [l_x])
-    m_s = mm(0, T.qr[:], T.sr[:], T.q1[:], T.s1[:], C, [p_u, p_us, q_x])
+    a_k2 = act(k2_, sg_, 2.0, K, [a_sg])
     keep["jm"] = act(T.jm[:], j16, S, b1_, [a_b1])
-    a_jb2 = act(T.jb2[:, 0:24], T.j2[:], K, k2_, [a_k2, g_j2])
+    a_jb2 = act(T.jb2[:, 0:24], T.j2[:], 1.0, k2_, [a_k2, g_j2])
     v_4 = spread_a("1", v_3)
-    q_e += [q_eb(2), q_eb(3)]
+    q_e.append(q_eb(3))
     v_5 = spread_b("1", v_4)
 
     def unpack(q, s, m, banks, deps):
@@ -234,11 +241,11 @@ def rank_program(g, core, T, topo):
     def evac(f, lo, m, banks, evs):
         return [act(f[:, 4 * lo + b:4 * (lo + m):4], bank(banks[b], 0, m), 0.5, None, [evs[b]]) for b in range(4)]
 
-    def flag(lo, step, in_, w, deps):
-        return ts(T.fb[:, w * (C + 1) + lo:w * (C + 1) + C:step], in_, 0.0, K + w, AL.is_gt, AL.mult, deps)
+    def flag(lo, hi, in_, w, deps):
+        return ts(T.fb[:, w * (C + 1) + lo:w * (C + 1) + hi], in_, 0.0, K + w, AL.is_gt, AL.mult, deps)
 
-    def count(deps):
-        return scan(T.ys[:], T.fb[:, C:2 * C], T.fb[:, 0:C], K, AL.add, AL.subtract, deps)
+    def count(lo, hi, deps):
+        return scan(T.ys[:, lo:hi], T.fb[:, C + lo:C + hi], T.fb[:, lo:hi], K, AL.add, AL.subtract, deps)
 
     def hold(out, steps_, data, deps):
         return scan(out, steps_, data, 0.0, AL.add, AL.max, deps)
@@ -253,7 +260,11 @@ def rank_program(g, core, T, topo):
 
     mb = [5, 6, 7, 0]
 
-    def layer(r, sc, fdeps, mdeps, bdeps, hook, q, s, k):
+    def send(k, q, s, land, own, m, sem, deps):
+        push(k, q[:, land:land + m].bitcast(dt.uint8), q[:, own:own + m].bitcast(dt.uint8), sem, deps)
+        push(k, s[:, land:land + m], s[:, own:own + m], sem, deps)
+
+    def layer(r, sc, fdeps, mdeps, bdeps, hook, q, s, at):
         w, hw, im, fm = T["w" + r], T["hw" + r], T["im" + r], T["fm" + r]
         ol, oh, om = T["ol" + r], T["oh" + r], T["om" + r]
         f, fh, p, pp, z, t, vt = [T[x + r] for x in ("f", "fh", "p", "pp", "z", "t", "vt")]
@@ -264,17 +275,21 @@ def rank_program(g, core, T, topo):
         sl = scan(hw[:, 0:H], T.d4[:], w[:, 0:C:2], 0.0, AL.add, AL.max, [sc])
         hook("held", None)
         oh_ = ts(oh[:], hw[:, H + 3:C:4], c4_, 1.0 / AW, AL.add, AL.mult, [sh, keep["c4"]])
-        gh = [act(fh[:, 256 * j:256 * j + 256], f[:].indirect(oh[:, 16 * j:16 * j + 16]), 1.0, None, [oh_] + fdeps) for j in range(3)]
+        cu = [0, 8, 32, 48]
+        gh = [None] + [act(fh[:, 16 * cu[j]:16 * cu[j + 1]], f[:].indirect(oh[:, cu[j]:cu[j + 1]]), 1.0, None, [oh_] + fdeps) for j in (1, 2)]
         hook("right", None)
         i2 = ts(im[:, 1:96:2], hw[:, H + 3:C:4], 31, None, AL.bitwise_and, None, [sh])
+        hook("right list", [sh])
         i1 = ts(im[:, 0:96:2], hw[:, 3:H:4], 3, 124, AL.logical_shift_right, AL.bitwise_and, [sl])
         ol_ = ts(ol[:], hw[:, 3:H:4], c4_, 1.0 / AW, AL.add, AL.mult, [sl])
-        hook("lists", [sh, sl])
+        gh[0] = cp(fh[:, 0:16 * cu[1]], f[:].indirect(oh[:, 0:cu[1]]), [oh_] + fdeps)
+        hook("lists", [sl])
         i3 = scan(fm[:], T.five[:], im[:], 0.0, AL.mult, AL.add, [i1, i2, g_5])
         hook("sum", None)
 
         def most(j):
-            return tt(p[:, 256 * j:256 * j + 256], f[:].indirect(ol[:, 16 * j:16 * j + 16]), fh[:, 256 * j:256 * j + 256], AL.max, [ol_, gh[j]] + fdeps)
+            return tt(p[:, 16 * cu[j]:16 * cu[j + 1]], f[:].indirect(ol[:, cu[j]:cu[j + 1]]), fh[:, 16 * cu[j]:16 * cu[j + 1]], AL.max,
+                      [ol_, gh[j]] + fdeps)
 
         def weights(banks, lo, deps):
             return [mm(banks[b], T.qw[:, 128 * b:128 * b + 128], T.sw[:, 128 * b:128 * b + 128], qz[:, lo:lo + 128], sz[:, lo:lo + 128], 128,
@@ -290,6 +305,7 @@ def rank_program(g, core, T, topo):
         hook("most 1", None)
         pa = act(pp[:, 0:a4], p[:, 0:a4], 64.0, None, mx)
         mx.append(most(2))
+        hook("most 2", None)
         pb = act(pp[:, a4:h4], p[:, a4:h4], 64.0, None, [mx[2]])
         za = tt(z[:, 0:a4], T.mf[:].indirect(om[:, 0:NA // 4]), p[:, 0:a4], AL.add, mx[0:2] + [om_] + mdeps)
         zb = tt(z[:, a4:h4], T.mf[:].indirect(om[:, NA // 4:H // 4]), p[:, a4:h4], AL.add, [mx[2]])
@@ -301,12 +317,10 @@ def rank_program(g, core, T, topo):
         sv = [act(vt[:, b:a4:4], t[:, b:a4:4], 0.03125, None, [ad[b]]) for b in range(4)]
         bd = plus(mb, 128 - (H - NA), a4, h4, rb, pb)
         hook("added", None)
-        sv.append(ts(vt[:, a4:h4], t[:, a4:h4], 0.03125, None, AL.mult, None, bd))
-        hook("scaled", None)
-        va = quant(q[:, H:C], s[:, H:C], vt[:], sv)
-        push(k, q[:, 0:H].bitcast(dt.uint8), q[:, H:C].bitcast(dt.uint8), "rq" + r, [va])
-        push(k, s[:, 0:H], s[:, H:C], "rq" + r, [va])
-        return va
+        sb = ts(vt[:, a4:h4], t[:, a4:h4], 0.03125, None, AL.mult, None, bd)
+        va = quant(q[:, at:at + 128], s[:, at:at + 128], vt[:, 0:512], sv)
+        hook("packed", va)
+        return va, quant(q[:, at + 128:at + 256], s[:, at + 128:at + 256], vt[:, h4 - 512:h4], [sb])
 
     e_m = []
 
@@ -315,69 +329,90 @@ def rank_program(g, core, T, topo):
         q_m = quant(T.qm[:, lo:lo + m], T.sm[:, lo:lo + m], T.ms[:, 4 * lo:4 * (lo + m)], [l_m[k]])
         e_m.extend(evac(T.mf, lo, m, mb, unpack(T.qm[:, lo:lo + m], T.sm[:, lo:lo + m], m, mb, [d + [q_m] for d in deps])))
 
+    m_d = unpack(T.q1[:], T.s1[:], C, [1, 2, 3, 4], [[]] * 4)
+    e_f = [act(T.f1[:, 0:4 * C:4], bank(1, 0, C), 0.5, None, [m_d[0]])]
+    f1 = [flag(H * h, H * h + H, bank(5 * h, 0, H), 0, [m_s[h]]) for h in range(2)]
     v_6 = spread_c("1", v_5)
     a_x = act(T.xg1[:], T.tc1[:].indirect(offx), 1.0, is_, [v_6, c_u, a_is])
-    e_f = evac(T.f1, 0, C, [1, 2, 3, 4], unpack(T.q1[:], T.s1[:], C, [1, 2, 3, 4], [[]] * 4))
-    f1 = [flag(0, 1, bank(0, 0, C), w, [m_s]) for w in range(2)]
-    n1 = total(T.sm1[:, 72:73], T.fb[:, 0:C], [f1[0]])
-    s1 = count(f1 + [z_f])
+    e_f += [act(T.f1[:, b:4 * C:4], bank(1 + b, 0, C), 0.5, None, [m_d[b]]) for b in (1, 2, 3)]
+    f1 += [flag(H * h, H * h + H, bank(5 * h, 0, H), 1, [m_s[h]]) for h in range(2)]
+    n1 = total(T.sm1[:, 72:73], T.fb[:, 0:C], f1[0:2])
+    s1 = count(0, C, f1 + [z_f])
     mid(0, [f1] * 4)
-    h1 = hold(T.yh1[:], T.d16[:], T.ys[:], [s1] + a_d16)
     jt = ts(T.sm1[:, 0:24], T.jb1[:], T.sm1[:, 72:73], 1.0 / K, AL.add, AL.mult, [n1, a_jb1])
-    mid(1, [[e] for e in e_m])
+    h1 = hold(T.yh1[:], T.d16[:], T.ys[:], [s1] + a_d16)
+    v_t = [turn(T.val1[:, 0:H], T.xg1[:, 0:H], [a_x])]
 
     def fills1(k):
         if k == 0:
-            keep["vt"] = turn(T.val1[:], T.xg1[:], [a_x])
-        return [keep["vt"]]
+            v_t.append(turn(T.val1[:, H:C], T.xg1[:, H:C], [a_x]))
+        else:
+            mid(1, [[e] for e in e_m])
+        return v_t
 
     sc = places("1", jt, [h1], fills1, T.val1[:])
 
     def hook1(at, held):
         if at == "lists":
             keep["xa"] = ts(T.xa[:, 0:48], T.hw1[:, 3:H:4], 31, None, AL.bitwise_and, None, held)
+        if at == "right list":
             keep["xb"] = ts(T.xa[:, 48:96], T.hw1[:, H + 3:C:4], 31 * 32, None, AL.bitwise_and, None, held)
-        if at == "sum":
-            keep["xs"] = tt(T.xb[:, 0:48], T.xa[:, 0:48], T.xa[:, 48:96], AL.add, [keep["xa"], keep["xb"]])
         if at == "most 0":
-            keep["xh"] = scan(T.xb[:, 48:96], T.d4t[:], T.xb[:, 0:48], 0.0, AL.add, AL.max, [keep["xs"], a_d4t])
+            keep["xs"] = tt(T.xb[:, 0:48], T.xa[:, 0:48], T.xa[:, 48:96], AL.add, [keep["xa"], keep["xb"]])
         if at == "most 1":
+            keep["xh"] = scan(T.xb[:, 48:96], T.d4t[:], T.xb[:, 0:48], 0.0, AL.add, AL.max, [keep["xs"], a_d4t])
+        if at == "most 2":
             push(0, T.xd[:], T.xc[:], "rl1", [tt(T.xc[:], T.xb[:, 51:96:4], T.jm[:, 0:12], AL.add, [keep["xh"], keep["jm"]])])
-        if at == "gap a":
-            keep["s0"] = ts(T.ee[:, 0:64], T.ic[:], sg_, None, AL.add, None, [g_c, a_sg])
         if at == "gap b":
             keep["o"] = [tt(T.ta2[:, 64 * h + 6:64 * h + 12], T.xb[:, 51 + 4 * h:96:8], T.jm[:, 12 + h:24:2], AL.add, [keep["xh"], z_t[1]])
                          for h in range(2)]
+        if at == "ordered":
+            keep["s0"] = ts(T.ee[:, 0:64], T.ic[:], sg_, None, AL.add, None, [g_c, a_sg])
+        if at == "held":
             keep["s1"] = ts(T.ee[:, 64:128], T.ee[:, 0:64], 15, None, AL.bitwise_and, None, [keep["s0"]])
-        if at == "added":
+        if at == "sum":
             keep["cp"] = ts(T.dp[:, 0:64], T.ee[:, 64:128], 0.0695, 128.465, AL.mult, AL.add, [keep["s1"]])
+        if at == "most 0":
+            keep["ds"] = steps(T.d16s, T.dp, H, square(T.dp, [keep["cp"]]))
+        if at == "gap a":
+            keep["ds"].append(act(T.d16s[:, H:C], T.d16s[:, 0:H], 1.0, None, keep["ds"]))
 
-    va1 = layer("1", sc, e_f, e_m, e_m, hook1, T.q2, T.s2, 0)
+    va1, vb1 = layer("1", sc, e_f, e_m, e_m, hook1, T.qs, T.ss, 0)
 
-    m_so = mm(5, T.qr[:], T.sr[:], T.q2[:, H:C], T.s2[:, H:C], H, [va1])
-    m_do = unpack(T.q2[:, H:C], T.s2[:, H:C], H, [1, 2, 3, 4], [[]] * 4)
-    a_ds = steps(T.d16s, T.dp, H, square(T.dp, [keep["cp"]]))
+    m_so = [mm(5 + h, T.qr[:], T.sr[:], T.qs[:, 128 * h:128 * h + 128], T.ss[:, 128 * h:128 * h + 128], 128, [v]) for h, v in enumerate((va1, vb1))]
+    v_1w = quant(T.q2[:, H:C], T.s2[:, H:C], T.vt1[:])
+    send(0, T.q2, T.s2, 0, H, H, "rq1", [v_1w])
+    m_do = unpack(T.q2[:, H:C], T.s2[:, H:C], H, [1, 2, 3, 4], [[v_1w]] * 4)
     o_a = [cp(T.ta2[:, 64 * h:64 * h + 6], T.xd[:, h:12:2], [("rl1", width(src[0])), z_t[1]]) for h in range(2)]
+    fo = [flag(0, NA, bank(5, 0, NA), w, [m_so[0]]) for w in range(2)]
+    fo += [flag(NA, H, bank(6, 128 - NB, 128), w, [m_so[1]]) for w in range(2)]
     o_4 = spread_a("2", o_a + keep["o"])
-    fo = [flag(1, 2, bank(5, 0, H), w, [m_so]) for w in range(2)]
-    o_5 = spread_b("2", o_4)
-    n2 = total(T.sm2[:, 73:74], T.fb[:, 1:C:2], [fo[0]])
-    o_6 = spread_c("2", o_5)
-    a_y = act(T.xg2[:], T.tc2[:].indirect(offx), 1.0, None, [o_6])
+    s2 = [count(0, H, fo), scan(T.ys[:, H:C], T.fb[:, C + 1:C + 1 + H], T.fb[:, 0:H], 0.0, AL.add, AL.subtract, fo)]
+    n2 = total(T.sm2[:, 72:73], T.fb[:, 0:H], [fo[0], fo[2]])
     e_o = evac(T.f2, H, H, [1, 2, 3, 4], m_do)
-    j_o = ts(T.jb2[:, 24:48], T.jb2[:, 0:24], T.sm2[:, 73:74], None, AL.add, None, [n2, a_jb2])
+    h2 = hold(T.yh2[:], T.d16s[:], T.ys[:], s2 + keep["ds"])
+    n3 = ts(T.sm2[:, 73:74], T.sm2[:, 72:73], 1.0 / K, nb_, AL.mult, AL.subtract, [n2])
+    o_5 = spread_b("2", o_4)
+    ca, cb, cc = T.ca, T.cb, T.cc
+    g_0 = ts(ca[:, 0:24], T.yh2[:, 15:C:16], nb_, None, AL.add, None, [h2])
+    g_1 = ts(ca[:, 24:48], T.yh2[:, 15:C:16], -1.0, T.sm2[:, 73:74], AL.mult, AL.add, [h2, n3])
+    push(0, cb[:], ca[:], "rc1", [g_0, g_1])
+    a_y = act(T.xg2[:], T.tc2[:].indirect(offx), 1.0, None, [spread_c("2", o_5)])
+    w_f = ts(cc[:, 48:60], ca[:, 0:12], K, None, AL.is_lt, None, [g_0])
+    w_t = tt(cc[:, 60:72], ca[:, 36:48], T.jb2[:, 0:12], AL.add, [g_1, a_jb2])
+    w_z = cp(cc[:, 12:24], ca[:, 0:12])
+    w_o = tt(cc[:, 36:48], ca[:, 24:36], T.jb2[:, 12:24], AL.add)
+    w_e = tt(cc[:, 0:12], ca[:, 12:24], cc[:, 48:60], AL.subtract, [w_f])
+    w_a = tt(cc[:, 24:36], cc[:, 60:72], cc[:, 48:60], AL.add, [w_t])
     v_u = turn(T.val2[:], T.xg2[:], [a_y])
 
     r1 = ("rq1", 2 * width(src[0]))
-    m_sa = mm(6, T.qr[:], T.sr[:], T.q2[:, 0:H], T.s2[:, 0:H], H, [r1])
-    l_v = dma("S", T.vs[:], T.v[:], [m_sa])
-    e_a = evac(T.f2, 0, H, [1, 2, 3, 4], unpack(T.q2[:, 0:H], T.s2[:, 0:H], H, [1, 2, 3, 4], [[e] for e in e_o]))
-    fa = [flag(0, 2, bank(6, 0, H), w, [m_sa]) for w in range(2)]
-    n3 = total(T.sm2[:, 72:73], T.fb[:, 0:C:2], [fa[0]])
-    s2 = count(fa + fo)
-    jt2 = ts(T.sm2[:, 0:24], T.jb2[:, 24:48], T.sm2[:, 72:73], 1.0 / K, AL.add, AL.mult, [n3, j_o])
-    h2 = [hold(T.yh2[:, H * k:H * k + H], T.d16s[:], T.ys[:, k:C:2], [s2] + a_ds) for k in range(2)]
-    sc2 = places("2", jt2, h2, lambda k: [v_u], T.val2[:])
+    m_da = unpack(T.q2[:, 0:H], T.s2[:, 0:H], H, [1, 2, 3, 4], [[e, r1] for e in e_o])
+    l_v = dma("S", T.vs[:], T.v[:], [m_da[0]])
+    e_a = evac(T.f2, 0, H, [1, 2, 3, 4], m_da)
+    w_s = tt(T.sm2[:, 0:48], cb[:], cc[:, 0:48], AL.add, [("rc1", width(src[0])), w_z, w_o, w_e, w_a])
+    po2 = tt(T.pos2[:], T.sm2[:, 0:24], T.sm2[:, 24:48], AL.min, [w_s])
+    sc2 = cp(T.w2[:].indirect(T.pos2[:]), T.val2[:], [po2, v_u])
 
     def hook2(at, held):
         if at == "ordered":
@@ -387,31 +422,44 @@ def rank_program(g, core, T, topo):
             keep["lw"] = dma("S", T.lw[:], T.wd[0:128:16, :], [keep["a0"], keep["a1"]])
             push(1, T.lwr[:], T.lw[:], "rl2", [keep["lw"]])
             a_h = act(ih_, ci_, 0.5)
-            keep["fq"] = act(fq_, co_, H - 0.5, ih_, [a_h])
+            a_g = act(ig_, ci_, 0.5, float(NB))
+            keep["fq"] = act(fq_, co_, NA - 0.5, ih_, [a_h])
+            keep["fr"] = act(fr_, co_, -NB - 0.5, ig_, [a_g])
         if at == "gap a":
-            keep["of"] = ts(T.offf[:], j16, 0.5, fq_, AL.mult, AL.add, [keep["fq"]])
+            keep["of"] = ts(T.offf[:, 0:16], T.jq[:, 24:40], 0.5, fq_, AL.mult, AL.add, [keep["fq"]])
+        if at == "packed":
+            send(1, T.q3, T.s3, 0, NA, NA, "ra2", [held])
         if at == "gap b":
+            keep["og"] = ts(T.offf[:, 16:24], T.jq[:, 24:32], 0.5, fr_, AL.mult, AL.add, [keep["fr"]])
             keep["qv"] = quant(T.qv[:], T.sv[:], T.vs[:], [l_v])
         if at == "added":
             keep["u0"] = ts(T.lri[:, 1:48:2], T.lw[:], lm_, -0.3, AL.mult, AL.add, [keep["lm"], keep["lw"]])
 
-    va2 = layer("2", sc2, e_o + e_a, [], [], hook2, T.q3, T.s3, 1)
+    va2, vb2 = layer("2", sc2, e_o + e_a, [], [], hook2, T.q3, T.s3, NA)
+    send(1, T.q3, T.s3, OB + NB, OB, NB, "rb2", [vb2])
 
+    ra2, rb2, a2 = ("ra2", 2 * width(src[1])), ("rb2", 2 * width(src[1])), 2 * NA
     done = []
-    m_yo = mm(5, T.qv[:], T.sv[:], T.q3[:, H:C], T.s3[:, H:C], H, [va2, keep["qv"]])
+    m_yo = mm(5, T.qv[:], T.sv[:], T.q3[:, NA:NA + 256], T.s3[:, NA:NA + 256], 256, [va2, vb2, keep["qv"]])
     u_1 = ts(T.lri[:, 0:48:2], T.lwr[:], lm_, -0.3, AL.mult, AL.add, [("rl2", width(src[1]))])
     u_2 = ts(T.lrj[:], T.lri[:], 31, None, AL.bitwise_and, None, [keep["u0"], u_1])
     u_3 = cp(T.lrf[:], T.lrj[:], [u_2])
-    done.append(dma("S", T.lr[:], T.lrf[:], [u_3]))
-    y_o = act(T.yb[:, 1:C:2], bank(5, 0, H), 1.0, None, [m_yo])
-    r2 = ("rq2", 2 * width(src[1]))
-    m_ya = mm(6, T.qv[:], T.sv[:], T.q3[:, 0:H], T.s3[:, 0:H], H, [r2, keep["qv"]])
-    p_s = act(T.so[:], T.s3[:].indirect(T.offf[:]), 1.0, None, [r2, va2, keep["of"]])
-    p_c = cp(T.qo[:].bitcast(dt.uint32), T.q3[:].bitcast(dt.uint32).indirect(T.offf[:]), [r2, va2, keep["of"]])
-    done.append(dma("S", T.oc[:], T.qo[:].bitcast(dt.uint8), [p_c]))
-    done.append(dma("S", T.y[:], T.yb[:], [cp(T.yb[:, 0:C:2], bank(6, 0, H), [m_ya]), y_o]))
+    done.append(dma("S", T.lr[:], T.lrf[:], [u_3, ra2]))
+    y_o = [act(T.yb[:, 1:a2:2], bank(5, 0, NA), 1.0, None, [m_yo]), act(T.yb[:, a2 + 1:C:2], bank(5, 256 - NB, 256), 1.0, None, [m_yo])]
+
+    def pick(lo, hi, wlo, whi, off, deps):
+        c = cp(T.qo[:, lo:hi].bitcast(dt.uint32), T.q3[:, wlo:whi].bitcast(dt.uint32).indirect(off), deps)
+        done.append(dma("S", T.oc[:, 4 * lo:4 * hi], T.qo[:, lo:hi].bitcast(dt.uint8), [c]))
+        return act(T.so[:, lo:hi], T.s3[:, wlo:whi].indirect(off), 1.0, None, deps)
+
+    m_ya = mm(6, T.qv[:], T.sv[:], T.q3[:, 0:NA], T.s3[:, 0:NA], NA, [ra2])
+    p_s = [pick(0, a2, 0, a2, T.offf[:, 0:16], [ra2, va2, keep["of"]])]
+    done.append(dma("S", T.y[:, 0:a2], T.yb[:, 0:a2], [cp(T.yb[:, 0:a2:2], bank(6, 0, NA), [m_ya]), y_o[0]]))
+    m_yb = mm(7, T.qv[:], T.sv[:], T.q3[:, QW - 128:QW], T.s3[:, QW - 128:QW], 128, [rb2])
+    p_s.append(pick(a2, C, OB, QW, T.offf[:, 16:24], [rb2, vb2, keep["og"]]))
+    done.append(dma("S", T.y[:, a2:C], T.yb[:, a2:C], [cp(T.yb[:, a2:C:2], bank(7, 128 - NB, 128), [m_yb]), y_o[1]]))
     for k in range(4):
-        done.append(dma("A" if k < 3 else "S", T.osc[4 * k:4 * k + 4, :], T.so[32 * k:32 * k + 4, :], [p_s]))
+        done.append(dma("A" if k < 3 else "S", T.osc[4 * k:4 * k + 4, :], T.so[32 * k:32 * k + 4, :], p_s))
     op("G", None, [("sent", sent[0])] + done, 0)
 
     known = {e: set() for e in queues}

from concourse.bass import DstId, RemoteDMATransfer
from concourse.mybir import dt, AluOpType, ActivationFunctionType, AxisListType

C = 384
H = C // 2
NA = 128
NB = H - NA
QW = 2 * NA + 128 + NB
OB = QW - 2 * NB
NM = 400
HALF = "float16"
X4 = "float8_e4m3fn_x4"
K = 512.0
B16 = 1024.0
L4 = 4194304.0
L1 = 1024.0
AW = 2048.0
S = 4 * AW


def _sb(n, d):
    return ("sbuf", [128, n], d)


SCRATCH = {
    "ps": ("psum", [128, 4096], "float32"),
    "xs": _sb(4 * C, "bfloat16"), "us": _sb(512, "bfloat16"), "vs": _sb(512, "bfloat16"), "ms": _sb(4 * NM, "bfloat16"),
    "q1": _sb(C, X4), "s1": _sb(C, "uint8"), "q2": _sb(C, X4), "s2": _sb(C, "uint8"), "q3": _sb(QW, X4), "s3": _sb(QW, "uint8"),
    "qs": _sb(256, X4), "ss": _sb(256, "uint8"),
    "qo": _sb(C, X4), "so": _sb(C, "uint8"),
    "qu": _sb(128, X4), "su": _sb(128, "uint8"), "qr": _sb(128, X4), "sr": _sb(128, "uint8"),
    "qv": _sb(128, X4), "sv": _sb(128, "uint8"), "qm": _sb(NM, X4), "sm": _sb(NM, "uint8"),
    "qw": _sb(512, X4), "sw": _sb(512, "uint8"), "qe": _sb(512, X4), "se": _sb(512, "uint8"),
    "eb": _sb(520, "bfloat16"),
    "ia": _sb(64, "int32"), "ib": _sb(64, "int32"), "ic": _sb(64, "int32"), "ea": _sb(64, "int32"), "ec": _sb(66, "int32"),
    "ed": _sb(64, "int32"), "ee": _sb(128, "int32"),
    "ds": _sb(128, "bfloat16"), "dm": _sb(64, "bfloat16"), "dn": _sb(64, "bfloat16"), "dp": _sb(128, "bfloat16"),
    "cf": _sb(4, "float32"), "cd": _sb(24, "float32"),
    "jq": _sb(48, "float32"), "j2": _sb(24, "float32"), "five": _sb(96, "float32"), "jm": _sb(24, "float32"),
    "d16": _sb(C, "bfloat16"), "d4": _sb(H, "bfloat16"), "d4t": _sb(48, "bfloat16"), "d16s": _sb(C, "bfloat16"),
    "offs": _sb(32, "uint16"), "offf": _sb(24, "uint16"),
    "lab": _sb(48, "int32"), "lt": _sb(48, "float32"), "jc": _sb(24, "float32"), "jb1": _sb(24, "float32"), "jb2": _sb(48, "float32"),
    "mf": _sb(4 * NM, "bfloat16"),
    "fb": _sb(2 * C + 2, HALF), "ys": _sb(C, HALF),
    "xa": _sb(96, "int32"), "xb": _sb(96, "float32"), "xc": _sb(12, "float32"), "xd": _sb(12, "float32"),
    "wd": _sb(C, "float32"), "lw": _sb(24, "float32"), "lwr": _sb(24, "float32"),
    "lri": _sb(48, "int32"), "lrj": _sb(48, "int32"), "lrf": _sb(48, "float32"),
    "yb": _sb(C, "float32"), "ca": _sb(48, HALF), "cb": _sb(48, HALF), "cc": _sb(72, "float32"),
}
for _r in ("1", "2"):
    SCRATCH.update({
        "ta" + _r: _sb(96, "float32"), "tb" + _r: _sb(96, "float32"), "tc" + _r: _sb(64, "float32"),
        "xg" + _r: _sb(C, "float32"), "val" + _r: _sb(C, "float32"), "w" + _r: _sb(C, "float32"),
        "f" + _r: _sb(4 * C, "bfloat16"), "yh" + _r: _sb(C, HALF),
        "sm" + _r: _sb(80, "float32"), "pos" + _r: _sb(24, "uint16"), "hw" + _r: _sb(C, "int32"),
        "ol" + _r: _sb(48, "uint16"), "oh" + _r: _sb(48, "uint16"), "om" + _r: _sb(48, "uint16"),
        "im" + _r: _sb(96, "int32"), "fm" + _r: _sb(96, "float32"),
        "fh" + _r: _sb(4 * H, "bfloat16"), "p" + _r: _sb(4 * H, "bfloat16"), "pp" + _r: _sb(4 * H, "bfloat16"),
        "z" + _r: _sb(4 * H, "bfloat16"), "t" + _r: _sb(4 * H, "bfloat16"), "vt" + _r: _sb(4 * H, "bfloat16"),
        "qz" + _r: _sb(256, X4), "sz" + _r: _sb(256, "uint8"),
    })
NSEM = 140
SEMAPHORES = ["e%d" % k for k in range(NSEM)] + ["rq1", "ra2", "rb2", "rl1", "rl2", "rc1", "sent"]

AL = AluOpType
AF = ActivationFunctionType


def rank_program(g, core, T, topo):
    rank = T.rank_of(core)
    if rank is None:
        return
    n = len(T.cores)
    queues = {"V": g.vector, "A": g.scalar, "P": g.tensor, "S": g.sync, "G": g}
    calls = []

    def op(e, call, deps=(), inc=1):
        calls.append((e, call, [d for d in deps if d is not None], inc))
        return len(calls) - 1

    def dma(e, out, in_, deps=()):
        return op(e, lambda q: q.dma_start(out, in_), deps, 16)

    def ts(out, in0, a, b, o0, o1=None, deps=()):
        if o1 is None:
            return op("V", lambda q: q.tensor_scalar(out, in0, a, None, o0), deps)
        return op("V", lambda q: q.tensor_scalar(out, in0, a, b, o0, o1), deps)

    def tt(out, in0, in1, o, deps=()):
        return op("V", lambda q: q.tensor_tensor(out, in0, in1, o), deps)

    def cp(out, in_, deps=()):
        return op("V", lambda q: q.tensor_copy(out, in_), deps)

    def turn(out, in_, deps=()):
        return op("V", lambda q: q.transpose(out, in_), deps)

    def total(out, in_, deps=()):
        return op("V", lambda q: q.tensor_reduce(out, in_, AxisListType.X, AL.add), deps)

    def scan(out, d0, d1, init, o0, o1, deps=()):
        return op("V", lambda q: q.tensor_tensor_scan(out, d0, d1, init, o0, o1), deps)

    def quant(out, sc, in_, deps=()):
        return op("V", lambda q: q.quantize_mx(out, sc, in_), deps)

    def fill(ap, c):
        return op("V", lambda q: q.memset(ap, c))

    def act(out, in_, scale=1.0, bias=None, deps=(), func=None):
        if bias is None:
            if isinstance(scale, float) and scale == 1.0:
                return op("A", lambda q: q.activation(out, in_, AF.Copy), deps)
            return op("A", lambda q: q.activation(out, in_, AF.Copy, scale=scale), deps)
        return op("A", lambda q: q.activation(out, in_, func or AF.Identity, bias=bias, scale=scale), deps)

    def mm(b, w, sw, x, sx, m, deps=()):
        return op("P", lambda q: q.matmul_mx(T.ps[:, 512 * b:512 * b + m], w, sw, x, sx, True, True), deps)

    def iota(out, pattern, base, cm, flt):
        if flt:
            return op("G", lambda q: q.iota(out, pattern, base, cm, allow_small_or_imprecise_dtypes=True))
        return op("G", lambda q: q.iota(out, pattern, base, cm))

    def bank(b, lo, hi):
        return T.ps[:, 512 * b + lo:512 * b + hi]

    dst = [T.cores[(rank + 1) % n], T.cores[(rank + 2) % n]]
    src = [T.cores[(rank - 1) % n], T.cores[(rank - 2) % n]]

    def lanes(c):
        r = T.rank_of(c)
        return topo.mask(c, T.cores[(r + 1) % n]) & topo.mask(c, T.cores[(r + 2) % n])

    def width(c):
        return bin(lanes(c)).count("1")

    sent = [0]

    def push(k, out, in_, sem, deps):
        rid, pid, _e = topo.addr(dst[k])
        op("G", lambda q: q.remote_dma(out, in_, T.sem[sem], T.sem["sent"], pid, rid, lanes(core)), deps, 0)
        sent[0] += width(core)

    l_u = dma("S", T.us[:], T.u[:])
    l_x = dma("S", T.xs[:], T.x[:])
    l_r = dma("A", T.lab[:, 24:48], T.ri[:])
    l_l = dma("A", T.lab[:, 0:24], T.li[:])
    cut = [0, NM // 2, NM]
    l_m = [dma("S", T.ms[:, 4 * cut[k]:4 * cut[k + 1]], T.mid[:, 4 * cut[k]:4 * cut[k + 1]], [l_u]) for k in range(2)]
    l_w = dma("S", T.qw[:].bitcast(dt.uint8), T.wc[:], [l_m[0]])
    l_ws = dma("S", T.sw[:], T.ws[:])

    z_e = fill(T.eb[:], 0.0)
    g_a = iota(T.ia[:], [[-1, 64]], 64, 1, False)
    g_j = iota(T.jq[:, 24:48], [[16, 24]], 0, 0, True)
    g_e = op("G", lambda q: q.affine_select(T.eb[:, 3:515:4], T.eb[:, 3:515:4], [[1, 128]], AL.not_equal, 1.0, 0, -1), [z_e])
    g_x = iota(T.jq[:, 0:24], [[1, 12], [-32, 2]], 32, 0, True)
    g_b = iota(T.ib[:], [[-4, 64]], 256, 1, False)
    g_j2 = iota(T.j2[:], [[1, 2], [32, 12]], 0, 0, True)
    g_5 = iota(T.five[:], [[0, 48], [5, 2]], 0, 0, True)
    g_c = iota(T.ic[:], [[-1, 64]], 64, 0, False)
    j16, offx, offu = T.jq[:, 24:48], T.offs[:, 0:24], T.offs[:, 24:32]
    ci_, cs_, co_ = T.cf[:, 0:1], T.cf[:, 2:3], T.cf[:, 3:4]
    mu_, nb_, is_, k0_, k1_, k2_, ct_, c3_, c4_, lm_, ih_, fq_, sg_, b0_, b1_, ig_, fr_ = [T.cd[:, k:k + 1] for k in range(17)]
    keep = {}

    def q_eb(b):
        return quant(T.qe[:, 128 * b:128 * b + 128], T.se[:, 128 * b:128 * b + 128], T.eb[:, 3 - b:515 - b], [g_e])

    def square(d, deps):
        return act(d[:, 64:128], d[:, 0:64], 1.0, -130.5, deps, AF.Square)

    def steps(out, d, m, sq):
        return [act(out[:, 64 * k:64 * k + 64], d[:, 64:128], -B16 / 2, 2.25 * B16 / 2, [sq]) for k in range(m // 64)]

    def spread_a(r, deps):
        return turn(T["tb" + r][:], T["ta" + r][:], deps)

    def spread_b(r, dep):
        tb = T["tb" + r]
        return [cp(tb[:, 32:48], tb[:, 80:96], [dep]), cp(tb[:, 48:64], tb[:, 0:16], [dep])]

    def spread_c(r, deps):
        return turn(T["tc" + r][:], T["tb" + r][:, 16:80], deps)

    z_t = [fill(T.ta1[:], 0.0), fill(T.ta2[:], 0.0)]
    z_f = fill(T.fb[:, C:C + 1], 0.0)
    c_a = ts(T.ea[:], T.ia[:], 15, None, AL.bitwise_and, None, [g_a])
    c_o = ts(T.ec[:, 64:65], T.ia[:, 0:1], 1, None, AL.bitwise_and)
    c_t = ts(T.ed[:, 0:48], T.ia[:, 0:48], 3, None, AL.bitwise_and)
    c_d = ts(T.ds[:, 0:64], T.ea[:], 0.0695, 128.465, AL.mult, AL.add, [c_a])
    c_c = cp(ci_, T.ea[:, 0:1], [c_a])
    c_n = ts(T.dn[:, 0:48], T.ed[:, 0:48], 1.0, None, AL.min, None, [c_t])
    a_jc = act(T.jc[:], j16, S, None, [g_j])
    a_mu = act(mu_, T.ds[:, 15:16], -1.0, 129.0, [c_d], AF.Relu)
    a_sq = square(T.ds, [c_d])
    a_is = act(is_, ci_, S, None, [c_c])
    a_c3 = act(c3_, ci_, AW, -3 * L4)
    a_d4t = act(T.d4t[:], T.dn[:, 0:48], 5 * L1, -4 * L1, [c_n])
    a_k0 = act(k0_, mu_, -K * B16, K * (K + B16), [a_mu])
    a_nb = act(nb_, mu_, B16, -B16, [a_mu])
    a_d16 = steps(T.d16, T.ds, H, a_sq)
    a_k1 = act(k1_, ci_, K, k0_, [a_k0])
    a_d16.append(act(T.d16[:, H:C], T.d16[:, 0:H], 1.0, None, a_d16))
    a_jb1 = act(T.jb1[:], j16, K, k1_, [a_k1])
    keep["lm"] = ts(lm_, ci_, 8.0, 1.0 / 32, AL.is_lt, AL.max, [c_c])
    q_e = [q_eb(0)]
    v_1 = ts(T.lt[:, 0:24], T.lab[:, 24:48], 32.0, None, AL.mult, None, [l_r])
    c_u = cp(T.offs[:], T.jq[:, 0:32], [g_j, g_x])
    q_e.append(q_eb(1))
    v_2 = tt(T.lt[:, 24:48], T.lab[:, 0:24], T.jc[:], AL.add, [l_l, a_jc])
    q_e.append(q_eb(2))
    c_b = ts(T.ec[:, 0:64], T.ib[:], 2, 3, AL.logical_shift_right, AL.bitwise_and, [g_b])
    q_u = quant(T.qu[:], T.su[:], T.us[:], [l_u])
    v_3 = [tt(T.ta1[:, 64 * h:64 * h + 12], T.lt[:, h:24:2], T.lt[:, 24 + h:48:2], AL.add, [v_1, v_2, z_t[0]]) for h in range(2)]
    c_2 = cp(T.cf[:, 2:4], T.ec[:, 0:65:64], [c_b, c_o])
    c_m = ts(T.dm[:], T.ec[:, 0:64], 1.0, None, AL.min, None, [c_b])
    p_u = cp(T.qr[:].bitcast(dt.uint32), T.qu[:].bitcast(dt.uint32).indirect(offu), [q_u, c_u])
    p_us = act(T.sr[:], T.su[:].indirect(offu), 1.0, None, [q_u, c_u])
    keep["ct"] = act(ct_, cs_, -4.0, ci_, [c_2])
    keep["c4"] = act(c4_, cs_, L4 - 4 * AW, c3_, [a_c3, c_2])
    keep["d4"] = [act(T.d4[:, 64 * j:64 * j + 64], T.dm[:], 5 * L4, -4 * L4, [c_m]) for j in range(H // 64)]
    a_sg = act(sg_, ct_, 4.0, cs_, [keep["ct"]])
    a_b0 = act(b0_, ct_, L1, -3 * L1, [keep["ct"]])
    m_s = []
    for h in range(2):
        q_x = quant(T.q1[:, H * h:H * h + H], T.s1[:, H * h:H * h + H], T.xs[:, 4 * H * h:4 * H * h + 4 * H], [l_x])
        m_s.append(mm(5 * h, T.qr[:], T.sr[:], T.q1[:, H * h:H * h + H], T.s1[:, H * h:H * h + H], H, [p_u, p_us, q_x]))
    a_b1 = act(b1_, sg_, S, b0_, [a_sg, a_b0])
    a_k2 = act(k2_, sg_, 2.0, K, [a_sg])
    keep["jm"] = act(T.jm[:], j16, S, b1_, [a_b1])
    a_jb2 = act(T.jb2[:, 0:24], T.j2[:], 1.0, k2_, [a_k2, g_j2])
    v_4 = spread_a("1", v_3)
    q_e.append(q_eb(3))
    v_5 = spread_b("1", v_4)

    def unpack(q, s, m, banks, deps):
        return [mm(banks[b], T.qe[:, 128 * b:128 * b + 128], T.se[:, 128 * b:128 * b + 128], q, s, m, deps[b] + [q_e[b]]) for b in range(4)]

    def evac(f, lo, m, banks, evs):
        return [act(f[:, 4 * lo + b:4 * (lo + m):4], bank(banks[b], 0, m), 0.5, None, [evs[b]]) for b in range(4)]

    def flag(lo, hi, in_, w, deps):
        return ts(T.fb[:, w * (C + 1) + lo:w * (C + 1) + hi], in_, 0.0, K + w, AL.is_gt, AL.mult, deps)

    def count(lo, hi, deps):
        return scan(T.ys[:, lo:hi], T.fb[:, C + lo:C + hi], T.fb[:, lo:hi], K, AL.add, AL.subtract, deps)

    def hold(out, steps_, data, deps):
        return scan(out, steps_, data, 0.0, AL.add, AL.max, deps)

    def places(r, jt, hs, fills, val):
        yh, sm = T["yh" + r], T["sm" + r]
        d = tt(sm[:, 24:48], sm[:, 0:24], yh[:, 15:C:16], AL.subtract, [jt] + hs)
        y0 = ts(sm[:, 48:72], yh[:, 15:C:16], nb_, None, AL.add, None, hs + [a_nb])
        fills(0)
        po = tt(T["pos" + r][:], sm[:, 24:48], sm[:, 48:72], AL.min, [d, y0])
        return cp(T["w" + r][:].indirect(T["pos" + r][:]), val, [po] + fills(1))

    mb = [5, 6, 7, 0]

    def send(k, q, s, land, own, m, sem, deps):
        push(k, q[:, land:land + m].bitcast(dt.uint8), q[:, own:own + m].bitcast(dt.uint8), sem, deps)
        push(k, s[:, land:land + m], s[:, own:own + m], sem, deps)

    def layer(r, sc, fdeps, mdeps, bdeps, hook, q, s, at):
        w, hw, im, fm = T["w" + r], T["hw" + r], T["im" + r], T["fm" + r]
        ol, oh, om = T["ol" + r], T["oh" + r], T["om" + r]
        f, fh, p, pp, z, t, vt = [T[x + r] for x in ("f", "fh", "p", "pp", "z", "t", "vt")]
        qz, sz = T["qz" + r], T["sz" + r]
        a4, h4 = 4 * NA, 4 * H
        hook("ordered", None)
        sh = scan(hw[:, H:C], T.d4[:], w[:, 1:C:2], 0.0, AL.add, AL.max, [sc] + keep["d4"])
        sl = scan(hw[:, 0:H], T.d4[:], w[:, 0:C:2], 0.0, AL.add, AL.max, [sc])
        hook("held", None)
        oh_ = ts(oh[:], hw[:, H + 3:C:4], c4_, 1.0 / AW, AL.add, AL.mult, [sh, keep["c4"]])
        cu = [0, 8, 32, 48]
        gh = [None] + [act(fh[:, 16 * cu[j]:16 * cu[j + 1]], f[:].indirect(oh[:, cu[j]:cu[j + 1]]), 1.0, None, [oh_] + fdeps) for j in (1, 2)]
        hook("right", None)
        i2 = ts(im[:, 1:96:2], hw[:, H + 3:C:4], 31, None, AL.bitwise_and, None, [sh])
        hook("right list", [sh])
        i1 = ts(im[:, 0:96:2], hw[:, 3:H:4], 3, 124, AL.logical_shift_right, AL.bitwise_and, [sl])
        ol_ = ts(ol[:], hw[:, 3:H:4], c4_, 1.0 / AW, AL.add, AL.mult, [sl])
        gh[0] = cp(fh[:, 0:16 * cu[1]], f[:].indirect(oh[:, 0:cu[1]]), [oh_] + fdeps)
        hook("lists", [sl])
        i3 = scan(fm[:], T.five[:], im[:], 0.0, AL.mult, AL.add, [i1, i2, g_5])
        hook("sum", None)

        def most(j):
            return tt(p[:, 16 * cu[j]:16 * cu[j + 1]], f[:].indirect(ol[:, cu[j]:cu[j + 1]]), fh[:, 16 * cu[j]:16 * cu[j + 1]], AL.max,
                      [ol_, gh[j]] + fdeps)

        def weights(banks, lo, deps):
            return [mm(banks[b], T.qw[:, 128 * b:128 * b + 128], T.sw[:, 128 * b:128 * b + 128], qz[:, lo:lo + 128], sz[:, lo:lo + 128], 128,
                       deps + [l_w, l_ws]) for b in range(4)]

        def plus(banks, at, lo, hi, rr, dep):
            return [tt(t[:, lo + b:hi:4], bank(banks[b], at, 128), pp[:, lo + b:hi:4], AL.add, [rr[b], dep]) for b in range(4)]

        mx = [most(0)]
        om_ = ts(om[:], fm[:, 1:96:2], 4.0, ct_, AL.mult, AL.add, [i3, keep["ct"]])
        hook("most 0", None)
        mx.append(most(1))
        hook("most 1", None)
        pa = act(pp[:, 0:a4], p[:, 0:a4], 64.0, None, mx)
        mx.append(most(2))
        hook("most 2", None)
        pb = act(pp[:, a4:h4], p[:, a4:h4], 64.0, None, [mx[2]])
        za = tt(z[:, 0:a4], T.mf[:].indirect(om[:, 0:NA // 4]), p[:, 0:a4], AL.add, mx[0:2] + [om_] + mdeps)
        zb = tt(z[:, a4:h4], T.mf[:].indirect(om[:, NA // 4:H // 4]), p[:, a4:h4], AL.add, [mx[2]])
        ra = weights([1, 2, 3, 4], 0, [quant(qz[:, 0:128], sz[:, 0:128], z[:, 0:512], [za])])
        hook("gap a", None)
        rb = weights(mb, 128, [quant(qz[:, 128:256], sz[:, 128:256], z[:, h4 - 512:h4], [zb])] + bdeps)
        hook("gap b", None)
        ad = plus([1, 2, 3, 4], 0, 0, a4, ra, pa)
        sv = [act(vt[:, b:a4:4], t[:, b:a4:4], 0.03125, None, [ad[b]]) for b in range(4)]
        bd = plus(mb, 128 - (H - NA), a4, h4, rb, pb)
        hook("added", None)
        sb = ts(vt[:, a4:h4], t[:, a4:h4], 0.03125, None, AL.mult, None, bd)
        va = quant(q[:, at:at + 128], s[:, at:at + 128], vt[:, 0:512], sv)
        hook("packed", va)
        return va, quant(q[:, at + 128:at + 256], s[:, at + 128:at + 256], vt[:, h4 - 512:h4], [sb])

    e_m = []

    def mid(k, deps):
        lo, m = cut[k], cut[k + 1] - cut[k]
        q_m = quant(T.qm[:, lo:lo + m], T.sm[:, lo:lo + m], T.ms[:, 4 * lo:4 * (lo + m)], [l_m[k]])
        e_m.extend(evac(T.mf, lo, m, mb, unpack(T.qm[:, lo:lo + m], T.sm[:, lo:lo + m], m, mb, [d + [q_m] for d in deps])))

    m_d = unpack(T.q1[:], T.s1[:], C, [1, 2, 3, 4], [[]] * 4)
    e_f = [act(T.f1[:, 0:4 * C:4], bank(1, 0, C), 0.5, None, [m_d[0]])]
    f1 = [flag(H * h, H * h + H, bank(5 * h, 0, H), 0, [m_s[h]]) for h in range(2)]
    v_6 = spread_c("1", v_5)
    a_x = act(T.xg1[:], T.tc1[:].indirect(offx), 1.0, is_, [v_6, c_u, a_is])
    e_f += [act(T.f1[:, b:4 * C:4], bank(1 + b, 0, C), 0.5, None, [m_d[b]]) for b in (1, 2, 3)]
    f1 += [flag(H * h, H * h + H, bank(5 * h, 0, H), 1, [m_s[h]]) for h in range(2)]
    n1 = total(T.sm1[:, 72:73], T.fb[:, 0:C], f1[0:2])
    s1 = count(0, C, f1 + [z_f])
    mid(0, [f1] * 4)
    jt = ts(T.sm1[:, 0:24], T.jb1[:], T.sm1[:, 72:73], 1.0 / K, AL.add, AL.mult, [n1, a_jb1])
    h1 = hold(T.yh1[:], T.d16[:], T.ys[:], [s1] + a_d16)
    v_t = [turn(T.val1[:, 0:H], T.xg1[:, 0:H], [a_x])]

    def fills1(k):
        if k == 0:
            v_t.append(turn(T.val1[:, H:C], T.xg1[:, H:C], [a_x]))
        else:
            mid(1, [[e] for e in e_m])
        return v_t

    sc = places("1", jt, [h1], fills1, T.val1[:])

    def hook1(at, held):
        if at == "lists":
            keep["xa"] = ts(T.xa[:, 0:48], T.hw1[:, 3:H:4], 31, None, AL.bitwise_and, None, held)
        if at == "right list":
            keep["xb"] = ts(T.xa[:, 48:96], T.hw1[:, H + 3:C:4], 31 * 32, None, AL.bitwise_and, None, held)
        if at == "most 0":
            keep["xs"] = tt(T.xb[:, 0:48], T.xa[:, 0:48], T.xa[:, 48:96], AL.add, [keep["xa"], keep["xb"]])
        if at == "most 1":
            keep["xh"] = scan(T.xb[:, 48:96], T.d4t[:], T.xb[:, 0:48], 0.0, AL.add, AL.max, [keep["xs"], a_d4t])
        if at == "most 2":
            push(0, T.xd[:], T.xc[:], "rl1", [tt(T.xc[:], T.xb[:, 51:96:4], T.jm[:, 0:12], AL.add, [keep["xh"], keep["jm"]])])
        if at == "gap b":
            keep["o"] = [tt(T.ta2[:, 64 * h + 6:64 * h + 12], T.xb[:, 51 + 4 * h:96:8], T.jm[:, 12 + h:24:2], AL.add, [keep["xh"], z_t[1]])
                         for h in range(2)]
        if at == "ordered":
            keep["s0"] = ts(T.ee[:, 0:64], T.ic[:], sg_, None, AL.add, None, [g_c, a_sg])
        if at == "held":
            keep["s1"] = ts(T.ee[:, 64:128], T.ee[:, 0:64], 15, None, AL.bitwise_and, None, [keep["s0"]])
        if at == "sum":
            keep["cp"] = ts(T.dp[:, 0:64], T.ee[:, 64:128], 0.0695, 128.465, AL.mult, AL.add, [keep["s1"]])
        if at == "most 0":
            keep["ds"] = steps(T.d16s, T.dp, H, square(T.dp, [keep["cp"]]))
        if at == "gap a":
            keep["ds"].append(act(T.d16s[:, H:C], T.d16s[:, 0:H], 1.0, None, keep["ds"]))

    va1, vb1 = layer("1", sc, e_f, e_m, e_m, hook1, T.qs, T.ss, 0)

    m_so = [mm(5 + h, T.qr[:], T.sr[:], T.qs[:, 128 * h:128 * h + 128], T.ss[:, 128 * h:128 * h + 128], 128, [v]) for h, v in enumerate((va1, vb1))]
    v_1w = quant(T.q2[:, H:C], T.s2[:, H:C], T.vt1[:])
    send(0, T.q2, T.s2, 0, H, H, "rq1", [v_1w])
    m_do = unpack(T.q2[:, H:C], T.s2[:, H:C], H, [1, 2, 3, 4], [[v_1w]] * 4)
    o_a = [cp(T.ta2[:, 64 * h:64 * h + 6], T.xd[:, h:12:2], [("rl1", width(src[0])), z_t[1]]) for h in range(2)]
    fo = [flag(0, NA, bank(5, 0, NA), w, [m_so[0]]) for w in range(2)]
    fo += [flag(NA, H, bank(6, 128 - NB, 128), w, [m_so[1]]) for w in range(2)]
    o_4 = spread_a("2", o_a + keep["o"])
    s2 = [count(0, H, fo), scan(T.ys[:, H:C], T.fb[:, C + 1:C + 1 + H], T.fb[:, 0:H], 0.0, AL.add, AL.subtract, fo)]
    n2 = total(T.sm2[:, 72:73], T.fb[:, 0:H], [fo[0], fo[2]])
    e_o = evac(T.f2, H, H, [1, 2, 3, 4], m_do)
    h2 = hold(T.yh2[:], T.d16s[:], T.ys[:], s2 + keep["ds"])
    n3 = ts(T.sm2[:, 73:74], T.sm2[:, 72:73], 1.0 / K, nb_, AL.mult, AL.subtract, [n2])
    o_5 = spread_b("2", o_4)
    ca, cb, cc = T.ca, T.cb, T.cc
    g_0 = ts(ca[:, 0:24], T.yh2[:, 15:C:16], nb_, None, AL.add, None, [h2])
    g_1 = ts(ca[:, 24:48], T.yh2[:, 15:C:16], -1.0, T.sm2[:, 73:74], AL.mult, AL.add, [h2, n3])
    push(0, cb[:], ca[:], "rc1", [g_0, g_1])
    a_y = act(T.xg2[:], T.tc2[:].indirect(offx), 1.0, None, [spread_c("2", o_5)])
    w_f = ts(cc[:, 48:60], ca[:, 0:12], K, None, AL.is_lt, None, [g_0])
    w_t = tt(cc[:, 60:72], ca[:, 36:48], T.jb2[:, 0:12], AL.add, [g_1, a_jb2])
    w_z = cp(cc[:, 12:24], ca[:, 0:12])
    w_o = tt(cc[:, 36:48], ca[:, 24:36], T.jb2[:, 12:24], AL.add)
    w_e = tt(cc[:, 0:12], ca[:, 12:24], cc[:, 48:60], AL.subtract, [w_f])
    w_a = tt(cc[:, 24:36], cc[:, 60:72], cc[:, 48:60], AL.add, [w_t])
    v_u = turn(T.val2[:], T.xg2[:], [a_y])

    r1 = ("rq1", 2 * width(src[0]))
    m_da = unpack(T.q2[:, 0:H], T.s2[:, 0:H], H, [1, 2, 3, 4], [[e, r1] for e in e_o])
    l_v = dma("S", T.vs[:], T.v[:], [m_da[0]])
    e_a = evac(T.f2, 0, H, [1, 2, 3, 4], m_da)
    w_s = tt(T.sm2[:, 0:48], cb[:], cc[:, 0:48], AL.add, [("rc1", width(src[0])), w_z, w_o, w_e, w_a])
    po2 = tt(T.pos2[:], T.sm2[:, 0:24], T.sm2[:, 24:48], AL.min, [w_s])
    sc2 = cp(T.w2[:].indirect(T.pos2[:]), T.val2[:], [po2, v_u])

    def hook2(at, held):
        if at == "ordered":
            keep["a0"] = act(T.wd[:, 0:H], T.w2[:, 0:C:2], 1.0, None, [sc2])
            keep["a1"] = act(T.wd[:, H:C], T.w2[:, 1:C:2], 1.0, None, [sc2])
        if at == "right":
            keep["lw"] = dma("S", T.lw[:], T.wd[0:128:16, :], [keep["a0"], keep["a1"]])
            push(1, T.lwr[:], T.lw[:], "rl2", [keep["lw"]])
            a_h = act(ih_, ci_, 0.5)
            a_g = act(ig_, ci_, 0.5, float(NB))
            keep["fq"] = act(fq_, co_, NA - 0.5, ih_, [a_h])
            keep["fr"] = act(fr_, co_, -NB - 0.5, ig_, [a_g])
        if at == "gap a":
            keep["of"] = ts(T.offf[:, 0:16], T.jq[:, 24:40], 0.5, fq_, AL.mult, AL.add, [keep["fq"]])
        if at == "packed":
            send(1, T.q3, T.s3, 0, NA, NA, "ra2", [held])
        if at == "gap b":
            keep["og"] = ts(T.offf[:, 16:24], T.jq[:, 24:32], 0.5, fr_, AL.mult, AL.add, [keep["fr"]])
            keep["qv"] = quant(T.qv[:], T.sv[:], T.vs[:], [l_v])
        if at == "added":
            keep["u0"] = ts(T.lri[:, 1:48:2], T.lw[:], lm_, -0.3, AL.mult, AL.add, [keep["lm"], keep["lw"]])

    va2, vb2 = layer("2", sc2, e_o + e_a, [], [], hook2, T.q3, T.s3, NA)
    send(1, T.q3, T.s3, OB + NB, OB, NB, "rb2", [vb2])

    ra2, rb2, a2 = ("ra2", 2 * width(src[1])), ("rb2", 2 * width(src[1])), 2 * NA
    done = []
    m_yo = mm(5, T.qv[:], T.sv[:], T.q3[:, NA:NA + 256], T.s3[:, NA:NA + 256], 256, [va2, vb2, keep["qv"]])
    u_1 = ts(T.lri[:, 0:48:2], T.lwr[:], lm_, -0.3, AL.mult, AL.add, [("rl2", width(src[1]))])
    u_2 = ts(T.lrj[:], T.lri[:], 31, None, AL.bitwise_and, None, [keep["u0"], u_1])
    u_3 = cp(T.lrf[:], T.lrj[:], [u_2])
    done.append(dma("S", T.lr[:], T.lrf[:], [u_3, ra2]))
    y_o = [act(T.yb[:, 1:a2:2], bank(5, 0, NA), 1.0, None, [m_yo]), act(T.yb[:, a2 + 1:C:2], bank(5, 256 - NB, 256), 1.0, None, [m_yo])]

    def pick(lo, hi, wlo, whi, off, deps):
        c = cp(T.qo[:, lo:hi].bitcast(dt.uint32), T.q3[:, wlo:whi].bitcast(dt.uint32).indirect(off), deps)
        done.append(dma("S", T.oc[:, 4 * lo:4 * hi], T.qo[:, lo:hi].bitcast(dt.uint8), [c]))
        return act(T.so[:, lo:hi], T.s3[:, wlo:whi].indirect(off), 1.0, None, deps)

    m_ya = mm(6, T.qv[:], T.sv[:], T.q3[:, 0:NA], T.s3[:, 0:NA], NA, [ra2])
    p_s = [pick(0, a2, 0, a2, T.offf[:, 0:16], [ra2, va2, keep["of"]])]
    done.append(dma("S", T.y[:, 0:a2], T.yb[:, 0:a2], [cp(T.yb[:, 0:a2:2], bank(6, 0, NA), [m_ya]), y_o[0]]))
    m_yb = mm(7, T.qv[:], T.sv[:], T.q3[:, QW - 128:QW], T.s3[:, QW - 128:QW], 128, [rb2])
    p_s.append(pick(a2, C, OB, QW, T.offf[:, 16:24], [rb2, vb2, keep["og"]]))
    done.append(dma("S", T.y[:, a2:C], T.yb[:, a2:C], [cp(T.yb[:, a2:C:2], bank(7, 128 - NB, 128), [m_yb]), y_o[1]]))
    for k in range(4):
        done.append(dma("A" if k < 3 else "S", T.osc[4 * k:4 * k + 4, :], T.so[32 * k:32 * k + 4, :], p_s))
    op("G", None, [("sent", sent[0])] + done, 0)

    known = {e: set() for e in queues}
    behind, waits, needed = [], [], set()
    for e, call, deps, inc in calls:
        mine = []
        for d in sorted(set(deps), key=lambda x: -x if isinstance(x, int) else 1):
            if d not in known[e]:
                mine.append(d)
                needed.add(d)
                known[e].add(d)
                if isinstance(d, int):
                    known[e].update(behind[d])
        waits.append(mine)
        behind.append(set(known[e]))
    pool = {e: [] for e in queues}
    event, used = {}, [0]
    for j, (e, call, deps, inc) in enumerate(calls):
        for d in waits[j]:
            name, c = event[d] if isinstance(d, int) else d
            queues[e].wait_ge(T.sem[name], c)
        if call is None:
            continue
        ins = call(queues[e])
        if j in needed:
            free = [x for x in pool[e] if x[2] in behind[j]] if inc == 1 else []
            if free:
                slot = free[0]
            else:
                slot = ["e%d" % used[0], 0, j]
                used[0] += 1
                if inc == 1:
                    pool[e].append(slot)
            slot[1] += inc
            slot[2] = j
            ins.then_inc(T.sem[slot[0]], inc)
            event[j] = (slot[0], slot[1])
